import numpy as np
import ml_dtypes


def mxq(x, axis, fmt="e4m3"):
    dtype, down = {"e4m3": (ml_dtypes.float8_e4m3fn, 7), "e5m2": (ml_dtypes.float8_e5m2, 14)}[fmt]
    v = np.moveaxis(np.asarray(x, np.float32).astype(ml_dtypes.bfloat16).astype(np.float64), axis, -1)
    blocks = v.reshape(v.shape[:-1] + (-1, 32))
    amax = np.abs(blocks).max(-1, keepdims=True)
    byte = np.maximum(np.where(amax > 0, np.frexp(amax)[1] - 1 + 127, 0) - down, 1)
    scale = np.exp2(byte - 127.0)
    codes = (blocks / scale).astype(np.float32).astype(dtype).astype(np.float64)
    return np.moveaxis((codes * scale).reshape(v.shape), -1, axis)


WIDE = False


def mx_kscale(k):
    if not WIDE:
        return np.ones(k)
    levels = np.array([10, -10, 5, -5, 0])
    if k % 512:
        return np.exp2(np.random.permutation(np.resize(levels, k // 32))).repeat(32)
    a = np.empty((k // 512, 16))
    for p in range(k // 512):
        a[p, :8] = np.random.permutation(np.resize(levels, 8))
        for g in range(8):
            far = levels[np.abs(levels - a[p, g]) >= 10]
            a[p, g + 8] = far[np.random.randint(len(far))]
    return np.exp2(a.ravel()).repeat(32)


def f64(x):
    return np.asarray(x).astype(np.float64)


def striped(idx):
    return np.tile(idx.reshape(-1, 16).T, (8, 1)).astype(np.uint16)


def unstriped(offs):
    return offs[:16].T.reshape(-1).astype(np.int64)


E2M1 = np.array([0.0, 0.5, 1.0, 1.5, 2.0, 3.0, 4.0, 6.0, -0.0, -0.5, -1.0, -1.5, -2.0, -3.0, -4.0, -6.0])


def pack_weight(w, fmt):
    k, n = w.shape
    w = f64(np.asarray(w, np.float32).astype(ml_dtypes.bfloat16)).reshape(k // 32, 32, n)
    amax = np.abs(w).max(1)
    if fmt == "e4m3":
        byte = np.frexp(amax)[1] - 1 + 127 - 7
    else:
        mant, ex = np.frexp(amax / 6.0)
        byte = np.where(mant > 0.5, ex, ex - 1) + 127
    byte = np.clip(np.where(amax > 0, byte, 1), 1, 254)
    scaled = (w * np.exp2(127.0 - byte)[:, None, :]).reshape(k, n).astype(np.float32)
    by_word = np.ascontiguousarray(scaled.reshape(k // 512, 128, 4, n).transpose(0, 1, 3, 2))
    if fmt == "e4m3":
        words = by_word.astype(ml_dtypes.float8_e4m3fn).view(np.uint8)
    else:
        c = by_word.astype(ml_dtypes.float4_e2m1fn).view(np.uint8) & 0xF
        words = (c[..., 0::2] | (c[..., 1::2] << 4)).reshape(k // 512, 128, 2 * n)
    return np.ascontiguousarray(words), np.ascontiguousarray(byte.astype(np.uint8).reshape(k // 512, 16, n))


def unpack_weight(words, scales, fmt):
    g, _, n = scales.shape
    words = np.ascontiguousarray(words).reshape(g, 128, n, -1)
    if fmt == "e4m3":
        vals = words.view(ml_dtypes.float8_e4m3fn).astype(np.float64)
    else:
        nib = np.empty((g, 128, n, 4), np.uint8)
        nib[..., 0::2] = words & 0xF
        nib[..., 1::2] = words >> 4
        vals = E2M1[nib]
    vals = vals * np.repeat(np.exp2(scales.astype(np.float64) - 127.0), 8, axis=1)[..., None]
    return vals.transpose(0, 1, 3, 2).reshape(g * 512, n)


def silu(v):
    return v / (1.0 + np.exp(-np.maximum(v, -700.0)))


K, T, S, H, N = 512, 2048, 1024, 512, 256


def setup_inputs():
    n = np.random.standard_normal
    s = mx_kscale(K)
    u = mx_kscale(H)
    hard = np.random.permutation(T)[:S]
    x = pack_weight(n((K, T)) * s[:, None], "e4m3")
    w = pack_weight(n((K, N)) / np.sqrt(K) / s[:, None], "e4m3")
    w1 = pack_weight(n((K, H)) / np.sqrt(K) / s[:, None], "e4m3")
    w3 = pack_weight(n((K, H)) / np.sqrt(K) / s[:, None] * u, "e4m3")
    w2 = pack_weight(n((H, N)) / np.sqrt(H) / u[:, None], "e4m3")
    return {
        "x_words": x[0],
        "x_scales": x[1],
        "w_words": w[0],
        "w_scales": w[1],
        "w1_words": w1[0],
        "w1_scales": w1[1],
        "w3_words": w3[0],
        "w3_scales": w3[1],
        "w2_words": w2[0],
        "w2_scales": w2[1],
        "offs": striped(hard),
    }


def reference(x_words, x_scales, w_words, w_scales, w1_words, w1_scales, w3_words, w3_scales, w2_words, w2_scales, offs):
    w = unpack_weight(w_words, w_scales, "e4m3")
    w1 = unpack_weight(w1_words, w1_scales, "e4m3")
    w3 = unpack_weight(w3_words, w3_scales, "e4m3")
    w2 = unpack_weight(w2_words, w2_scales, "e4m3")
    idx = unstriped(offs)
    x = unpack_weight(x_words, x_scales, "e4m3")
    out = w.T @ x
    h = silu(w1.T @ x[:, idx]) * (w3.T @ x[:, idx])
    out[:, idx] = w2.T @ mxq(h, 0, "e4m3")
    return out

@@ -1,0 +1,182 @@
+from contextlib import ExitStack
+
+import concourse.mybir as mybir
+
+K, T, S, H, N = 512, 2048, 1024, 512, 256
+FLOPS = 2 * K * N * T + 2 * 2 * K * H * S + 2 * H * N * S
+
+F32 = mybir.dt.float32
+BF16 = mybir.dt.bfloat16
+I32 = mybir.dt.int32
+U32 = mybir.dt.uint32
+U16 = mybir.dt.uint16
+U8 = mybir.dt.uint8
+FP8X4 = mybir.dt.float8_e4m3fn_x4
+SILU = mybir.ActivationFunctionType.Silu
+MULT = mybir.AluOpType.mult
+
+P = 128
+PACK = 4
+BANK = 512
+TILE = 128
+CHUNK = 256
+PER_COLUMN = 16
+
+
+def load_words(queue, tile, words):
+    queue.dma_start(out=tile[:], in_=words[0].rearrange("p n d -> p (n d)").bitcast(I32))
+
+
+def load_scales(queue, tile, first_row, first_col, scales):
+    width = scales.shape[2]
+    for q in range(4):
+        rows = slice(32 * q + first_row, 32 * q + first_row + 4)
+        queue.dma_start(
+            out=tile[rows, first_col : first_col + width].bitcast(I32),
+            in_=scales[0, 4 * q : 4 * q + 4, :].bitcast(I32),
+        )
+
+
+def tile_moe_cas_glu_silu_kernel(
+    tc, x_words, x_scales, w_words, w_scales, w1_words, w1_scales, w3_words, w3_scales, w2_words, w2_scales, offs, out
+):
+    nc = tc.nc
+    with ExitStack() as ctx:
+        keep = ctx.enter_context(tc.tile_pool(name="keep", bufs=1))
+        ring = ctx.enter_context(tc.tile_pool(name="ring", bufs=4))
+        psum_a = ctx.enter_context(tc.psum_pool(name="psum_a", bufs=2))
+        psum_b = ctx.enter_context(tc.psum_pool(name="psum_b", bufs=3))
+        psum_o = ctx.enter_context(tc.psum_pool(name="psum_o", bufs=3))
+
+        offsets = keep.tile([P, S // PER_COLUMN], U16, name="offsets")
+        x_w = keep.tile([P, T], I32, name="x_w", align_bytes=64)
+        x_s = keep.tile([P, T], U8, name="x_s", align_bytes=64)
+        w_w = keep.tile([P, N], I32, name="w_w", align_bytes=64)
+        w2_w = keep.tile([P, N], I32, name="w2_w", align_bytes=64)
+        w1_raw = keep.tile([P, H], I32, name="w1_raw", align_bytes=64)
+        w3_raw = keep.tile([P, H], I32, name="w3_raw", align_bytes=64)
+        w1_w = keep.tile([P, H], I32, name="w1_w", align_bytes=64)
+        w3_w = keep.tile([P, H], I32, name="w3_w", align_bytes=64)
+        ws_raw = keep.tile([P, H + 2 * N], U8, name="ws_raw", align_bytes=64)
+        w13_s = keep.tile([P, H], U8, name="w13_s", align_bytes=64)
+        g_w = keep.tile([P, S], U32, name="g_w", align_bytes=64)
+        g_s = keep.tile([P, S], U8, name="g_s", align_bytes=64)
+        h_w = keep.tile([P, S], U32, name="h_w", align_bytes=64)
+        h_s = keep.tile([P, S], U8, name="h_s", align_bytes=64)
+        z = keep.tile([P, N // P, S], F32, name="z")
+        result = [keep.tile([P, T], F32, name="result%d" % n) for n in range(N // P)]
+
+        nc.vector.memset(x_s[:].bitcast(I32), 0)
+        nc.vector.memset(ws_raw[:].bitcast(I32), 0)
+        nc.sync.dma_start(offsets[:], offs)
+        load_words(nc.sync, w1_raw, w1_words)
+        load_words(nc.sync, w3_raw, w3_words)
+        load_words(nc.gpsimd, w_w, w_words)
+        load_words(nc.gpsimd, x_w, x_words)
+        load_scales(nc.scalar, x_s, 0, 0, x_scales)
+        load_scales(nc.sync, ws_raw, 0, 0, w1_scales)
+        load_scales(nc.sync, ws_raw, 4, 0, w3_scales)
+        load_scales(nc.sync, ws_raw, 0, H, w_scales)
+        load_scales(nc.sync, ws_raw, 0, H + N, w2_scales)
+        load_words(nc.gpsimd, w2_w, w2_words)
+
+        def offset_columns(first, count):
+            return offsets[:, first // PER_COLUMN : (first + count) // PER_COLUMN]
+
+        def gather_words(c):
+            nc.vector.tensor_copy(
+                g_w[:, c * CHUNK : (c + 1) * CHUNK],
+                x_w[:].bitcast(U32).indirect(offset_columns(c * CHUNK, CHUNK)),
+            )
+
+        def light_layer(n, banks):
+            for b in banks:
+                cols = slice(b * BANK, (b + 1) * BANK)
+                y = psum_o.tile([P, BANK], F32, name="o_bank", tag="o_bank")
+                nc.tensor.matmul_mx(
+                    out=y[:],
+                    lhsT=w_w[:, n * P : (n + 1) * P].bitcast(FP8X4),
+                    lhsT_scale=ws_raw[:, H + n * P : H + (n + 1) * P],
+                    rhs=x_w[:, cols].bitcast(FP8X4),
+                    rhs_scale=x_s[:, cols],
+                    start=True,
+                    stop=True,
+                )
+                nc.scalar.copy(result[n][:, cols], y[:])
+
+        def first_layer(tile, h):
+            cols = slice(tile * TILE, (tile + 1) * TILE)
+            a = psum_a.tile([P, PACK, TILE], F32, name="a_bank")
+            b = psum_b.tile([P, PACK, TILE], F32, name="b_bank")
+            for bank, words, row in ((a, w1_w, 0), (b, w3_w, 4)):
+                for t in range(PACK):
+                    nc.tensor.matmul_mx(
+                        out=bank[:, t, :],
+                        lhsT=words[:, t * P : (t + 1) * P].bitcast(FP8X4),
+                        lhsT_scale=w13_s[row:P, t * P : (t + 1) * P],
+                        rhs=g_w[:, cols].bitcast(FP8X4),
+                        rhs_scale=g_s[:, cols],
+                        start=True,
+                        stop=True,
+                    )
+            s = ring.tile([P, TILE, PACK], F32, name="s")
+            nc.scalar.activation(s[:], a[:].rearrange("p t j -> p j t"), SILU)
+            nc.vector.tensor_tensor(h, b[:].rearrange("p t j -> p j t"), s[:], MULT)
+
+        def quantise(c, h):
+            cols = slice(c * CHUNK, (c + 1) * CHUNK)
+            nc.vector.quantize_mx(
+                out=h_w[:, cols].bitcast(FP8X4), scales=h_s[:, cols], in_=h[:].rearrange("p j t -> p (j t)")
+            )
+
+        def second_layer(c):
+            cols = slice(c * CHUNK, (c + 1) * CHUNK)
+            o = psum_o.tile([P, N // P, CHUNK], F32, name="o_bank", tag="o_bank")
+            for n in range(N // P):
+                nc.tensor.matmul_mx(
+                    out=o[:, n, :],
+                    lhsT=w2_w[:, n * P : (n + 1) * P].bitcast(FP8X4),
+                    lhsT_scale=ws_raw[:, H + N + n * P : H + N + (n + 1) * P],
+                    rhs=h_w[:, cols].bitcast(FP8X4),
+                    rhs_scale=h_s[:, cols],
+                    start=True,
+                    stop=True,
+                )
+            nc.scalar.copy(z[:, :, cols], o[:])
+
+        nc.vector.tensor_copy(g_s[:], x_s[:].indirect(offsets[:]))
+        for raw, words in ((w1_raw, w1_w), (w3_raw, w3_w)):
+            nc.vector.tensor_copy(
+                words[:].rearrange("p (t m) -> p m t", t=PACK), raw[:].rearrange("p (m t) -> p m t", t=PACK)
+            )
+        nc.vector.tensor_copy(
+            w13_s[:].rearrange("p (t m) -> p t m", t=PACK), ws_raw[:, 0:H].rearrange("p (m t) -> p t m", t=PACK)
+        )
+        light_layer(0, range(0, 2))
+        for c in range(S // CHUNK):
+            gather_words(c)
+
+        hs = []
+        tiles_per_chunk = CHUNK // TILE
+        for c in range(S // CHUNK + 1):
+            if c < S // CHUNK:
+                h = ring.tile([P, CHUNK, PACK], BF16, name="h", align_bytes=64)
+                hs.append(h)
+                first_layer(c * tiles_per_chunk, h[:, 0:TILE, :])
+            if c > 0:
+                quantise(c - 1, hs[c - 1])
+            if c < S // CHUNK:
+                first_layer(c * tiles_per_chunk + 1, h[:, TILE:CHUNK, :])
+            if c == 0:
+                light_layer(0, range(2, 4))
+            if c > 0:
+                second_layer(c - 1)
+        light_layer(1, range(4))
+
+        for c in range(S // CHUNK):
+            nc.vector.tensor_copy(
+                result[0][:].indirect(offset_columns(c * CHUNK, CHUNK)), z[:, 0, c * CHUNK : (c + 1) * CHUNK]
+            )
+        nc.sync.dma_start(out=out[0:P, :], in_=result[0][:])
+        nc.vector.tensor_copy(result[1][:].indirect(offsets[:]), z[:, 1, :])
+        nc.sync.dma_start(out=out[P : 2 * P, :], in_=result[1][:])

@@ -27,9 +27,9 @@ def load_words(queue, tile, words):
     queue.dma_start(out=tile[:], in_=words[0].rearrange("p n d -> p (n d)").bitcast(I32))
 
 
-def load_scales(queue, tile, first_row, first_col, scales):
+def load_scales(queue, tile, first_row, first_col, scales, quadrants=range(4)):
     width = scales.shape[2]
-    for q in range(4):
+    for q in quadrants:
         rows = slice(32 * q + first_row, 32 * q + first_row + 4)
         queue.dma_start(
             out=tile[rows, first_col : first_col + width].bitcast(I32),
@@ -44,9 +44,8 @@ def tile_moe_cas_glu_silu_kernel(
     with ExitStack() as ctx:
         keep = ctx.enter_context(tc.tile_pool(name="keep", bufs=1))
         ring = ctx.enter_context(tc.tile_pool(name="ring", bufs=4))
-        psum_a = ctx.enter_context(tc.psum_pool(name="psum_a", bufs=2))
-        psum_b = ctx.enter_context(tc.psum_pool(name="psum_b", bufs=3))
-        psum_o = ctx.enter_context(tc.psum_pool(name="psum_o", bufs=3))
+        psum_s = ctx.enter_context(tc.psum_pool(name="psum_s", bufs=4))
+        psum_b = ctx.enter_context(tc.psum_pool(name="psum_b", bufs=4))
 
         offsets = keep.tile([P, S // PER_COLUMN], U16, name="offsets")
         x_w = keep.tile([P, T], I32, name="x_w", align_bytes=64)
@@ -68,17 +67,20 @@ def tile_moe_cas_glu_silu_kernel(
 
         nc.vector.memset(x_s[:].bitcast(I32), 0)
         nc.vector.memset(ws_raw[:].bitcast(I32), 0)
+        warm = keep.tile([P, 2], F32, name="warm")
+        nc.gpsimd.memset(warm[:, 0:1], 0.0)
+        nc.scalar.activation(warm[:, 1:2], warm[:, 0:1], SILU)
         nc.sync.dma_start(offsets[:], offs)
         load_words(nc.sync, w1_raw, w1_words)
         load_words(nc.sync, w3_raw, w3_words)
-        load_words(nc.gpsimd, w_w, w_words)
-        load_words(nc.gpsimd, x_w, x_words)
-        load_scales(nc.scalar, x_s, 0, 0, x_scales)
+        load_scales(nc.sync, x_s, 0, 0, x_scales)
+        load_words(nc.sync, x_w, x_words)
+        load_words(nc.sync, w_w, w_words)
+        load_scales(nc.sync, ws_raw, 0, H, w_scales)
         load_scales(nc.sync, ws_raw, 0, 0, w1_scales)
         load_scales(nc.sync, ws_raw, 4, 0, w3_scales)
-        load_scales(nc.sync, ws_raw, 0, H, w_scales)
+        load_words(nc.sync, w2_w, w2_words)
         load_scales(nc.sync, ws_raw, 0, H + N, w2_scales)
-        load_words(nc.gpsimd, w2_w, w2_words)
 
         def offset_columns(first, count):
             return offsets[:, first // PER_COLUMN : (first + count) // PER_COLUMN]
@@ -92,7 +94,7 @@ def tile_moe_cas_glu_silu_kernel(
         def light_layer(n, banks):
             for b in banks:
                 cols = slice(b * BANK, (b + 1) * BANK)
-                y = psum_o.tile([P, BANK], F32, name="o_bank", tag="o_bank")
+                y = psum_s.tile([P, BANK], F32, name="s_bank")
                 nc.tensor.matmul_mx(
                     out=y[:],
                     lhsT=w_w[:, n * P : (n + 1) * P].bitcast(FP8X4),
@@ -106,7 +108,7 @@ def tile_moe_cas_glu_silu_kernel(
 
         def first_layer(tile, h):
             cols = slice(tile * TILE, (tile + 1) * TILE)
-            a = psum_a.tile([P, PACK, TILE], F32, name="a_bank")
+            a = psum_s.tile([P, PACK, TILE], F32, name="s_bank")
             b = psum_b.tile([P, PACK, TILE], F32, name="b_bank")
             for bank, words, row in ((a, w1_w, 0), (b, w3_w, 4)):
                 for t in range(PACK):
@@ -129,49 +131,48 @@ def tile_moe_cas_glu_silu_kernel(
                 out=h_w[:, cols].bitcast(FP8X4), scales=h_s[:, cols], in_=h[:].rearrange("p j t -> p (j t)")
             )
 
-        def second_layer(c):
-            cols = slice(c * CHUNK, (c + 1) * CHUNK)
-            o = psum_o.tile([P, N // P, CHUNK], F32, name="o_bank", tag="o_bank")
-            for n in range(N // P):
-                nc.tensor.matmul_mx(
-                    out=o[:, n, :],
-                    lhsT=w2_w[:, n * P : (n + 1) * P].bitcast(FP8X4),
-                    lhsT_scale=ws_raw[:, H + N + n * P : H + N + (n + 1) * P],
-                    rhs=h_w[:, cols].bitcast(FP8X4),
-                    rhs_scale=h_s[:, cols],
-                    start=True,
-                    stop=True,
-                )
-            nc.scalar.copy(z[:, :, cols], o[:])
+        def second_layer(n, first, count):
+            cols = slice(first, first + count)
+            o = psum_s.tile([P, count], F32, name="s_bank")
+            nc.tensor.matmul_mx(
+                out=o[:],
+                lhsT=w2_w[:, n * P : (n + 1) * P].bitcast(FP8X4),
+                lhsT_scale=ws_raw[:, H + N + n * P : H + N + (n + 1) * P],
+                rhs=h_w[:, cols].bitcast(FP8X4),
+                rhs_scale=h_s[:, cols],
+                start=True,
+                stop=True,
+            )
+            nc.scalar.copy(z[:, n, cols], o[:])
 
-        nc.vector.tensor_copy(g_s[:], x_s[:].indirect(offsets[:]))
         for raw, words in ((w1_raw, w1_w), (w3_raw, w3_w)):
             nc.vector.tensor_copy(
                 words[:].rearrange("p (t m) -> p m t", t=PACK), raw[:].rearrange("p (m t) -> p m t", t=PACK)
             )
+        nc.vector.tensor_copy(g_s[:], x_s[:].indirect(offsets[:]))
         nc.vector.tensor_copy(
             w13_s[:].rearrange("p (t m) -> p t m", t=PACK), ws_raw[:, 0:H].rearrange("p (m t) -> p t m", t=PACK)
         )
-        light_layer(0, range(0, 2))
         for c in range(S // CHUNK):
             gather_words(c)
 
-        hs = []
+        light_layer(0, range(4))
+        hs = [keep.tile([P, CHUNK, PACK], BF16, name="h%d" % c, align_bytes=64) for c in range(S // CHUNK)]
         tiles_per_chunk = CHUNK // TILE
-        for c in range(S // CHUNK + 1):
-            if c < S // CHUNK:
-                h = ring.tile([P, CHUNK, PACK], BF16, name="h", align_bytes=64)
-                hs.append(h)
-                first_layer(c * tiles_per_chunk, h[:, 0:TILE, :])
-            if c > 0:
+        tiles = S // TILE
+        for tile in range(tiles):
+            c, half = divmod(tile, tiles_per_chunk)
+            first_layer(tile, hs[c][:, half * TILE : (half + 1) * TILE, :])
+            if half == 0 and c > 0:
                 quantise(c - 1, hs[c - 1])
-            if c < S // CHUNK:
-                first_layer(c * tiles_per_chunk + 1, h[:, TILE:CHUNK, :])
-            if c == 0:
-                light_layer(0, range(2, 4))
-            if c > 0:
-                second_layer(c - 1)
+            if half == 1 and c > 1:
+                second_layer(0, (c - 2) * CHUNK, CHUNK)
+        quantise(S // CHUNK - 1, hs[-1])
+        for c in range(S // CHUNK - 2, S // CHUNK):
+            second_layer(0, c * CHUNK, CHUNK)
         light_layer(1, range(4))
+        for first in range(0, S, BANK):
+            second_layer(1, first, BANK)
 
         for c in range(S // CHUNK):
             nc.vector.tensor_copy(
@@ -179,4 +180,5 @@ def tile_moe_cas_glu_silu_kernel(
             )
         nc.sync.dma_start(out=out[0:P, :], in_=result[0][:])
         nc.vector.tensor_copy(result[1][:].indirect(offsets[:]), z[:, 1, :])
-        nc.sync.dma_start(out=out[P : 2 * P, :], in_=result[1][:])
+        nc.sync.dma_start(out=out[P : 2 * P, 0 : T // 2], in_=result[1][:, 0 : T // 2])
+        nc.scalar.dma_start(out=out[P : 2 * P, T // 2 : T], in_=result[1][:, T // 2 : T])

@@ -21,6 +21,7 @@ BANK = 512
 TILE = 128
 CHUNK = 256
 PER_COLUMN = 16
+VECTOR_TILES = 5
 
 
 def load_words(queue, tile, words):
@@ -123,7 +124,12 @@ def tile_moe_cas_glu_silu_kernel(
                     )
             s = ring.tile([P, TILE, PACK], F32, name="s")
             nc.scalar.activation(s[:], a[:].rearrange("p t j -> p j t"), SILU)
-            nc.vector.tensor_tensor(h, b[:].rearrange("p t j -> p j t"), s[:], MULT)
+            if tile < VECTOR_TILES:
+                nc.vector.tensor_tensor(h, b[:].rearrange("p t j -> p j t"), s[:], MULT)
+            else:
+                u = ring.tile([P, TILE, PACK], F32, name="u")
+                nc.scalar.copy(u[:], b[:].rearrange("p t j -> p j t"))
+                nc.gpsimd.tensor_tensor(h, u[:], s[:], MULT)
 
         def quantise(c, h):
             cols = slice(c * CHUNK, (c + 1) * CHUNK)
@@ -158,26 +164,40 @@ def tile_moe_cas_glu_silu_kernel(
 
         light_layer(0, range(4))
         hs = [keep.tile([P, CHUNK, PACK], BF16, name="h%d" % c, align_bytes=64) for c in range(S // CHUNK)]
-        tiles_per_chunk = CHUNK // TILE
-        tiles = S // TILE
-        for tile in range(tiles):
-            c, half = divmod(tile, tiles_per_chunk)
-            first_layer(tile, hs[c][:, half * TILE : (half + 1) * TILE, :])
-            if half == 0 and c > 0:
-                quantise(c - 1, hs[c - 1])
-            if half == 1 and c > 1:
-                second_layer(0, (c - 2) * CHUNK, CHUNK)
-        quantise(S // CHUNK - 1, hs[-1])
-        for c in range(S // CHUNK - 2, S // CHUNK):
-            second_layer(0, c * CHUNK, CHUNK)
-        light_layer(1, range(4))
-        for first in range(0, S, BANK):
-            second_layer(1, first, BANK)
 
-        for c in range(S // CHUNK):
+        def token_tile(tile):
+            c, half = divmod(tile, CHUNK // TILE)
+            first_layer(tile, hs[c][:, half * TILE : (half + 1) * TILE, :])
+
+        def scatter_first(c):
             nc.vector.tensor_copy(
                 result[0][:].indirect(offset_columns(c * CHUNK, CHUNK)), z[:, 0, c * CHUNK : (c + 1) * CHUNK]
             )
+
+        for tile in range(3):
+            token_tile(tile)
+        quantise(0, hs[0])
+        token_tile(3)
+        token_tile(4)
+        quantise(1, hs[1])
+        second_layer(0, 0, CHUNK)
+        token_tile(5)
+        token_tile(6)
+        second_layer(0, CHUNK, CHUNK)
+        scatter_first(0)
+        quantise(2, hs[2])
+        token_tile(7)
+        light_layer(1, (0,))
+        second_layer(0, 2 * CHUNK, CHUNK)
+        scatter_first(1)
+        quantise(3, hs[3])
+        light_layer(1, (1, 2))
+        second_layer(1, 0, BANK)
+        second_layer(0, 3 * CHUNK, CHUNK)
+        light_layer(1, (3,))
+        second_layer(1, BANK, BANK)
+        scatter_first(2)
+        scatter_first(3)
         nc.sync.dma_start(out=out[0:P, :], in_=result[0][:])
         nc.vector.tensor_copy(result[1][:].indirect(offsets[:]), z[:, 1, :])
         nc.sync.dma_start(out=out[P : 2 * P, 0 : T // 2], in_=result[1][:, 0 : T // 2])

@@ -76,8 +76,8 @@ def tile_moe_cas_glu_silu_kernel(
         load_words(nc.sync, w3_raw, w3_words)
         load_scales(nc.sync, x_s, 0, 0, x_scales)
         load_words(nc.sync, x_w, x_words)
-        load_words(nc.sync, w_w, w_words)
         load_scales(nc.sync, ws_raw, 0, H, w_scales)
+        load_words(nc.sync, w_w, w_words)
         load_scales(nc.sync, ws_raw, 0, 0, w1_scales)
         load_scales(nc.sync, ws_raw, 4, 0, w3_scales)
         load_words(nc.sync, w2_w, w2_words)
@@ -163,16 +163,14 @@ def tile_moe_cas_glu_silu_kernel(
             gather_words(c)
 
         light_layer(0, range(4))
-        hs = [keep.tile([P, CHUNK, PACK], BF16, name="h%d" % c, align_bytes=64) for c in range(S // CHUNK)]
+        hs = [keep.tile([P, CHUNK, PACK], BF16, name="h%d" % c, align_bytes=64) for c in range(3)]
 
         def token_tile(tile):
             c, half = divmod(tile, CHUNK // TILE)
             first_layer(tile, hs[c][:, half * TILE : (half + 1) * TILE, :])
 
-        def scatter_first(c):
-            nc.vector.tensor_copy(
-                result[0][:].indirect(offset_columns(c * CHUNK, CHUNK)), z[:, 0, c * CHUNK : (c + 1) * CHUNK]
-            )
+        def scatter(n, first, count):
+            nc.vector.tensor_copy(result[n][:].indirect(offset_columns(first, count)), z[:, n, first : first + count])
 
         for tile in range(3):
             token_tile(tile)
@@ -182,23 +180,23 @@ def tile_moe_cas_glu_silu_kernel(
         quantise(1, hs[1])
         second_layer(0, 0, CHUNK)
         token_tile(5)
-        token_tile(6)
         second_layer(0, CHUNK, CHUNK)
-        scatter_first(0)
+        scatter(0, 0, CHUNK)
         quantise(2, hs[2])
+        hs.append(keep.tile([P, CHUNK, PACK], BF16, name="h2", align_bytes=64))
+        token_tile(6)
         token_tile(7)
-        light_layer(1, (0,))
         second_layer(0, 2 * CHUNK, CHUNK)
-        scatter_first(1)
-        quantise(3, hs[3])
-        light_layer(1, (1, 2))
+        light_layer(1, range(4))
         second_layer(1, 0, BANK)
+        scatter(0, CHUNK, CHUNK)
+        scatter(0, 2 * CHUNK, CHUNK)
+        quantise(3, hs[3])
         second_layer(0, 3 * CHUNK, CHUNK)
-        light_layer(1, (3,))
         second_layer(1, BANK, BANK)
-        scatter_first(2)
-        scatter_first(3)
+        scatter(1, 0, BANK)
+        scatter(0, 3 * CHUNK, CHUNK)
         nc.sync.dma_start(out=out[0:P, :], in_=result[0][:])
-        nc.vector.tensor_copy(result[1][:].indirect(offsets[:]), z[:, 1, :])
+        scatter(1, BANK, BANK)
         nc.sync.dma_start(out=out[P : 2 * P, 0 : T // 2], in_=result[1][:, 0 : T // 2])
         nc.scalar.dma_start(out=out[P : 2 * P, T // 2 : T], in_=result[1][:, T // 2 : T])

@@ -21,11 +21,10 @@ BANK = 512
 TILE = 128
 CHUNK = 256
 PER_COLUMN = 16
-VECTOR_TILES = 5
 
 
 def load_words(queue, tile, words):
-    queue.dma_start(out=tile[:], in_=words[0].rearrange("p n d -> p (n d)").bitcast(I32))
+    queue.dma_start(out=tile, in_=words[0].rearrange("p n d -> p (n d)").bitcast(I32))
 
 
 def load_scales(queue, tile, first_row, first_col, scales, quadrants=range(4)):
@@ -44,9 +43,8 @@ def tile_moe_cas_glu_silu_kernel(
     nc = tc.nc
     with ExitStack() as ctx:
         keep = ctx.enter_context(tc.tile_pool(name="keep", bufs=1))
-        ring = ctx.enter_context(tc.tile_pool(name="ring", bufs=4))
-        psum_s = ctx.enter_context(tc.psum_pool(name="psum_s", bufs=4))
-        psum_b = ctx.enter_context(tc.psum_pool(name="psum_b", bufs=4))
+        ring = ctx.enter_context(tc.tile_pool(name="ring", bufs=6))
+        psum = ctx.enter_context(tc.psum_pool(name="psum", bufs=1))
 
         offsets = keep.tile([P, S // PER_COLUMN], U16, name="offsets")
         x_w = keep.tile([P, T], I32, name="x_w", align_bytes=64)
@@ -57,146 +55,206 @@ def tile_moe_cas_glu_silu_kernel(
         w3_raw = keep.tile([P, H], I32, name="w3_raw", align_bytes=64)
         w1_w = keep.tile([P, H], I32, name="w1_w", align_bytes=64)
         w3_w = keep.tile([P, H], I32, name="w3_w", align_bytes=64)
-        ws_raw = keep.tile([P, H + 2 * N], U8, name="ws_raw", align_bytes=64)
-        w13_s = keep.tile([P, H], U8, name="w13_s", align_bytes=64)
-        g_w = keep.tile([P, S], U32, name="g_w", align_bytes=64)
+        ws = keep.tile([P, 2 * N + H], U8, name="ws", align_bytes=64)
+        w3s_raw = keep.tile([P, H], U8, name="stage", align_bytes=64)
+        w1_s = keep.tile([P, H], U8, name="w1_s", align_bytes=64)
+        w3_s = keep.tile([P, H], U8, name="w3_s", align_bytes=64)
         g_s = keep.tile([P, S], U8, name="g_s", align_bytes=64)
-        h_w = keep.tile([P, S], U32, name="h_w", align_bytes=64)
         h_s = keep.tile([P, S], U8, name="h_s", align_bytes=64)
-        z = keep.tile([P, N // P, S], F32, name="z")
         result = [keep.tile([P, T], F32, name="result%d" % n) for n in range(N // P)]
 
-        nc.vector.memset(x_s[:].bitcast(I32), 0)
-        nc.vector.memset(ws_raw[:].bitcast(I32), 0)
+        nc.vector.memset(x_s[:, 0 : T // 2].bitcast(I32), 0)
+        nc.gpsimd.memset(x_s[:, T // 2 : T].bitcast(I32), 0)
+        nc.vector.memset(ws[:].bitcast(I32), 0)
+        nc.vector.memset(w3s_raw[:].bitcast(I32), 0)
         warm = keep.tile([P, 2], F32, name="warm")
         nc.gpsimd.memset(warm[:, 0:1], 0.0)
         nc.scalar.activation(warm[:, 1:2], warm[:, 0:1], SILU)
+
+        x_dram = x_words[0].rearrange("p n d -> p (n d)").bitcast(I32)
         nc.sync.dma_start(offsets[:], offs)
-        load_words(nc.sync, w1_raw, w1_words)
-        load_words(nc.sync, w3_raw, w3_words)
+        load_words(nc.sync, w_w[:], w_words)
         load_scales(nc.sync, x_s, 0, 0, x_scales)
-        load_words(nc.sync, x_w, x_words)
-        load_scales(nc.sync, ws_raw, 0, H, w_scales)
-        load_words(nc.sync, w_w, w_words)
-        load_scales(nc.sync, ws_raw, 0, 0, w1_scales)
-        load_scales(nc.sync, ws_raw, 4, 0, w3_scales)
-        load_words(nc.sync, w2_w, w2_words)
-        load_scales(nc.sync, ws_raw, 0, H + N, w2_scales)
+        load_scales(nc.sync, ws, 0, 0, w_scales, range(0, 1))
+        nc.sync.dma_start(out=x_w[:, 0 : T // 2], in_=x_dram[:, 0 : T // 2])
+        load_scales(nc.sync, ws, 0, 0, w_scales, range(1, 4))
+        nc.sync.dma_start(out=x_w[:, T // 2 : T], in_=x_dram[:, T // 2 : T])
+        load_words(nc.sync, w1_raw[:], w1_words)
+        load_scales(nc.sync, ws, 0, 2 * N, w1_scales)
+        load_words(nc.sync, w3_raw[:], w3_words)
+        load_scales(nc.sync, w3s_raw, 0, 0, w3_scales, range(0, 1))
+        load_scales(nc.gpsimd, w3s_raw, 0, 0, w3_scales, range(1, 4))
+        load_scales(nc.sync, ws, 0, N, w2_scales)
+        load_words(nc.sync, w2_w[:], w2_words)
 
         def offset_columns(first, count):
             return offsets[:, first // PER_COLUMN : (first + count) // PER_COLUMN]
 
-        def gather_words(c):
-            nc.vector.tensor_copy(
-                g_w[:, c * CHUNK : (c + 1) * CHUNK],
-                x_w[:].bitcast(U32).indirect(offset_columns(c * CHUNK, CHUNK)),
+        def gather_words(out_words, c):
+            nc.vector.tensor_copy(out_words, x_w[:].bitcast(U32).indirect(offset_columns(c * CHUNK, CHUNK)))
+
+        def permute_words(engine, words, raw):
+            engine.tensor_copy(
+                words[:].rearrange("p (t c i) -> p c t i", t=PACK, i=PACK),
+                raw.rearrange("p (c i t) -> p c t i", t=PACK, i=PACK),
             )
 
-        def light_layer(n, banks):
-            for b in banks:
+        def permute_scales(engine, plane, raw):
+            engine.tensor_copy(
+                plane[:].rearrange("p (t m) -> p t m", t=PACK), raw.rearrange("p (m t) -> p t m", t=PACK)
+            )
+
+        def light_layer(n, b, bank, on_vector=False):
+            if True:
                 cols = slice(b * BANK, (b + 1) * BANK)
-                y = psum_s.tile([P, BANK], F32, name="s_bank")
+                y = psum.tile([P, BANK], F32, name="bank%d" % bank)
                 nc.tensor.matmul_mx(
                     out=y[:],
                     lhsT=w_w[:, n * P : (n + 1) * P].bitcast(FP8X4),
-                    lhsT_scale=ws_raw[:, H + n * P : H + (n + 1) * P],
+                    lhsT_scale=ws[:, n * P : (n + 1) * P],
                     rhs=x_w[:, cols].bitcast(FP8X4),
                     rhs_scale=x_s[:, cols],
                     start=True,
                     stop=True,
                 )
-                nc.scalar.copy(result[n][:, cols], y[:])
+                if on_vector:
+                    nc.vector.tensor_copy(result[n][:, cols], y[:])
+                else:
+                    nc.scalar.copy(result[n][:, cols], y[:])
 
-        def first_layer(tile, h):
-            cols = slice(tile * TILE, (tile + 1) * TILE)
-            a = psum_s.tile([P, PACK, TILE], F32, name="s_bank")
-            b = psum_b.tile([P, PACK, TILE], F32, name="b_bank")
-            for bank, words, row in ((a, w1_w, 0), (b, w3_w, 4)):
-                for t in range(PACK):
-                    nc.tensor.matmul_mx(
-                        out=bank[:, t, :],
-                        lhsT=words[:, t * P : (t + 1) * P].bitcast(FP8X4),
-                        lhsT_scale=w13_s[row:P, t * P : (t + 1) * P],
-                        rhs=g_w[:, cols].bitcast(FP8X4),
-                        rhs_scale=g_s[:, cols],
-                        start=True,
-                        stop=True,
-                    )
+        def first_layer_sums(bank, words, plane, tile):
+            for t in range(PACK):
+                nc.tensor.matmul_mx(
+                    out=bank[:, t, :],
+                    lhsT=words[:, t * P : (t + 1) * P].bitcast(FP8X4),
+                    lhsT_scale=plane[:, t * P : (t + 1) * P],
+                    rhs=g_w[tile].bitcast(FP8X4),
+                    rhs_scale=g_s[:, tile * TILE : (tile + 1) * TILE],
+                    start=True,
+                    stop=True,
+                )
+
+        def gate(tile, bank):
+            a = psum.tile([P, PACK, TILE], F32, name="bank%d" % bank)
+            first_layer_sums(a, w1_w, w1_s, tile)
             s = ring.tile([P, TILE, PACK], F32, name="s")
             nc.scalar.activation(s[:], a[:].rearrange("p t j -> p j t"), SILU)
-            if tile < VECTOR_TILES:
-                nc.vector.tensor_tensor(h, b[:].rearrange("p t j -> p j t"), s[:], MULT)
-            else:
-                u = ring.tile([P, TILE, PACK], F32, name="u")
-                nc.scalar.copy(u[:], b[:].rearrange("p t j -> p j t"))
-                nc.gpsimd.tensor_tensor(h, u[:], s[:], MULT)
+            return s
 
-        def quantise(c, h):
-            cols = slice(c * CHUNK, (c + 1) * CHUNK)
+        def product_on_vector(tile, s, h, bank):
+            b = psum.tile([P, PACK, TILE], F32, name="bank%d" % bank)
+            first_layer_sums(b, w3_w, w3_s, tile)
+            nc.vector.tensor_tensor(h, b[:].rearrange("p t j -> p j t"), s[:], MULT)
+
+        def value(tile, bank):
+            b = psum.tile([P, PACK, TILE], F32, name="bank%d" % bank)
+            first_layer_sums(b, w3_w, w3_s, tile)
+            u = ring.tile([P, TILE, PACK], F32, name="u")
+            nc.scalar.copy(u[:], b[:].rearrange("p t j -> p j t"))
+            return u
+
+        def product_on_gpsimd(s, u, h):
+            nc.gpsimd.tensor_tensor(h, u[:], s[:], MULT)
+
+        def quantise(first, count, h):
+            cols = slice(first, first + count)
+            words = h_w[first // CHUNK][:, first % CHUNK : first % CHUNK + count]
             nc.vector.quantize_mx(
-                out=h_w[:, cols].bitcast(FP8X4), scales=h_s[:, cols], in_=h[:].rearrange("p j t -> p (j t)")
+                out=words.bitcast(FP8X4), scales=h_s[:, cols], in_=h[:].rearrange("p j t -> p (j t)")
             )
 
-        def second_layer(n, first, count):
+        def second_layer(n, first, count, name, bank):
             cols = slice(first, first + count)
-            o = psum_s.tile([P, count], F32, name="s_bank")
+            z = keep.tile([P, count], F32, name=name, align_bytes=64)
+            o = psum.tile([P, count], F32, name="bank%d" % bank)
             nc.tensor.matmul_mx(
                 out=o[:],
                 lhsT=w2_w[:, n * P : (n + 1) * P].bitcast(FP8X4),
-                lhsT_scale=ws_raw[:, H + N + n * P : H + N + (n + 1) * P],
-                rhs=h_w[:, cols].bitcast(FP8X4),
+                lhsT_scale=ws[:, N + n * P : N + (n + 1) * P],
+                rhs=h_w[first // CHUNK][:].bitcast(FP8X4),
                 rhs_scale=h_s[:, cols],
                 start=True,
                 stop=True,
             )
-            nc.scalar.copy(z[:, n, cols], o[:])
+            nc.scalar.copy(z[:], o[:])
+            return z
 
-        for raw, words in ((w1_raw, w1_w), (w3_raw, w3_w)):
-            nc.vector.tensor_copy(
-                words[:].rearrange("p (t m) -> p m t", t=PACK), raw[:].rearrange("p (m t) -> p m t", t=PACK)
-            )
+        def scatter(n, first, count, z):
+            nc.vector.tensor_copy(result[n][:].indirect(offset_columns(first, count)), z[:])
+
+        def h_tile(name, tiles=1):
+            return keep.tile([P, tiles * TILE, PACK], BF16, name=name, align_bytes=64)
+
         nc.vector.tensor_copy(g_s[:], x_s[:].indirect(offsets[:]))
-        nc.vector.tensor_copy(
-            w13_s[:].rearrange("p (t m) -> p t m", t=PACK), ws_raw[:, 0:H].rearrange("p (m t) -> p t m", t=PACK)
-        )
-        for c in range(S // CHUNK):
-            gather_words(c)
+        g0 = keep.tile([P, CHUNK], U32, name="g0", align_bytes=64)
+        gather_words(g0[:], 0)
+        permute_words(nc.vector, w1_w, w1_raw[:])
+        permute_scales(nc.gpsimd, w1_s, ws[:, 2 * N : 2 * N + H])
+        g1 = keep.tile([P, CHUNK], U32, name="w1_raw", align_bytes=64)
+        gather_words(g1[:], 1)
+        permute_words(nc.gpsimd, w3_w, w3_raw[:])
+        permute_scales(nc.vector, w3_s, w3s_raw[:])
+        g23 = keep.tile([P, 2 * CHUNK], U32, name="stage", align_bytes=64)
+        gather_words(g23[:, 0:CHUNK], 2)
+        gather_words(g23[:, CHUNK : 2 * CHUNK], 3)
+        g_w = [g[:, j * TILE : (j + 1) * TILE] for g, k in ((g0, 2), (g1, 2), (g23, 4)) for j in range(k)]
 
-        light_layer(0, range(4))
-        hs = [keep.tile([P, CHUNK, PACK], BF16, name="h%d" % c, align_bytes=64) for c in range(3)]
-
-        def token_tile(tile):
-            c, half = divmod(tile, CHUNK // TILE)
-            first_layer(tile, hs[c][:, half * TILE : (half + 1) * TILE, :])
-
-        def scatter(n, first, count):
-            nc.vector.tensor_copy(result[n][:].indirect(offset_columns(first, count)), z[:, n, first : first + count])
-
-        for tile in range(3):
-            token_tile(tile)
-        quantise(0, hs[0])
-        token_tile(3)
-        token_tile(4)
-        quantise(1, hs[1])
-        second_layer(0, 0, CHUNK)
-        token_tile(5)
-        second_layer(0, CHUNK, CHUNK)
-        scatter(0, 0, CHUNK)
-        quantise(2, hs[2])
-        hs.append(keep.tile([P, CHUNK, PACK], BF16, name="h2", align_bytes=64))
-        token_tile(6)
-        token_tile(7)
-        second_layer(0, 2 * CHUNK, CHUNK)
-        light_layer(1, range(4))
-        second_layer(1, 0, BANK)
-        scatter(0, CHUNK, CHUNK)
-        scatter(0, 2 * CHUNK, CHUNK)
-        quantise(3, hs[3])
-        second_layer(0, 3 * CHUNK, CHUNK)
-        second_layer(1, BANK, BANK)
-        scatter(1, 0, BANK)
-        scatter(0, 3 * CHUNK, CHUNK)
+        for b in range(4):
+            light_layer(0, b, b)
+        light_layer(1, 0, 1)
+        s0 = gate(0, 4)
+        s1 = gate(1, 5)
+        s2 = gate(2, 0)
+        s3 = gate(3, 6)
+        h_w = [keep.tile([P, CHUNK], U32, name="h_w%d" % c, align_bytes=64) for c in range(4)]
+        h = [h_tile("h%d" % tile) for tile in range(4)]
+        product_on_vector(0, s0, h[0][:], 2)
+        product_on_vector(1, s1, h[1][:], 3)
+        quantise(0, TILE, h[0])
+        quantise(TILE, TILE, h[1])
+        product_on_vector(2, s2, h[2][:], 7)
+        product_on_vector(3, s3, h[3][:], 1)
+        z00 = second_layer(0, 0, CHUNK, "z00", 0)
+        light_layer(1, 1, 4)
+        light_layer(1, 2, 5)
+        light_layer(1, 3, 1)
+        quantise(2 * TILE, TILE, h[2])
+        quantise(3 * TILE, TILE, h[3])
+        scatter(0, 0, CHUNK, z00)
+        z10 = second_layer(1, 0, CHUNK, "z10", 6)
+        s4 = gate(4, 7)
+        u4 = value(4, 0)
+        h4 = h_tile("z00")
+        product_on_gpsimd(s4, u4, h4[:])
+        scatter(1, 0, CHUNK, z10)
+        quantise(4 * TILE, TILE, h4)
+        s5 = gate(5, 6)
+        u5 = value(5, 1)
+        z01 = second_layer(0, CHUNK, CHUNK, "z01", 0)
+        h5 = h_tile("z00")
+        product_on_gpsimd(s5, u5, h5[:])
+        scatter(0, CHUNK, CHUNK, z01)
+        quantise(5 * TILE, TILE, h5)
+        s6 = gate(6, 7)
+        u6 = value(6, 6)
+        z11 = second_layer(1, CHUNK, CHUNK, "z11", 1)
+        h6 = h_tile("z00")
+        product_on_gpsimd(s6, u6, h6[:])
+        scatter(1, CHUNK, CHUNK, z11)
+        quantise(6 * TILE, TILE, h6)
+        s7 = gate(7, 0)
+        u7 = value(7, 7)
+        z02 = second_layer(0, 2 * CHUNK, CHUNK, "z02", 4)
+        h7 = h_tile("z00")
+        product_on_gpsimd(s7, u7, h7[:])
+        scatter(0, 2 * CHUNK, CHUNK, z02)
+        quantise(7 * TILE, TILE, h7)
+        z12 = second_layer(1, 2 * CHUNK, CHUNK, "z12", 4)
+        scatter(1, 2 * CHUNK, CHUNK, z12)
+        z03 = second_layer(0, 3 * CHUNK, CHUNK, "z03", 5)
+        scatter(0, 3 * CHUNK, CHUNK, z03)
         nc.sync.dma_start(out=out[0:P, :], in_=result[0][:])
-        scatter(1, BANK, BANK)
+        z13 = second_layer(1, 3 * CHUNK, CHUNK, "z13", 4)
+        scatter(1, 3 * CHUNK, CHUNK, z13)
         nc.sync.dma_start(out=out[P : 2 * P, 0 : T // 2], in_=result[1][:, 0 : T // 2])
         nc.scalar.dma_start(out=out[P : 2 * P, T // 2 : T], in_=result[1][:, T // 2 : T])

@@ -60,7 +60,9 @@ def tile_moe_cas_glu_silu_kernel(
         w1_s = keep.tile([P, H], U8, name="w1_s", align_bytes=64)
         w3_s = keep.tile([P, H], U8, name="w3_s", align_bytes=64)
         g_s = keep.tile([P, S], U8, name="g_s", align_bytes=64)
+        h_w = keep.tile([P, S], U32, name="h_w", align_bytes=64)
         h_s = keep.tile([P, S], U8, name="h_s", align_bytes=64)
+        banks = [psum.tile([P, BANK], F32, name="bank%d" % b) for b in range(8)]
         result = [keep.tile([P, T], F32, name="result%d" % n) for n in range(N // P)]
 
         nc.vector.memset(x_s[:, 0 : T // 2].bitcast(I32), 0)
@@ -107,7 +109,7 @@ def tile_moe_cas_glu_silu_kernel(
         def light_layer(n, b, bank, on_vector=False):
             if True:
                 cols = slice(b * BANK, (b + 1) * BANK)
-                y = psum.tile([P, BANK], F32, name="bank%d" % bank)
+                y = banks[bank]
                 nc.tensor.matmul_mx(
                     out=y[:],
                     lhsT=w_w[:, n * P : (n + 1) * P].bitcast(FP8X4),
@@ -134,56 +136,57 @@ def tile_moe_cas_glu_silu_kernel(
                     stop=True,
                 )
 
-        def gate(tile, bank):
-            a = psum.tile([P, PACK, TILE], F32, name="bank%d" % bank)
+        def gate(tile, bank, pool=ring, name="s"):
+            a = banks[bank][:].rearrange("p (t j) -> p t j", t=PACK)
             first_layer_sums(a, w1_w, w1_s, tile)
-            s = ring.tile([P, TILE, PACK], F32, name="s")
-            nc.scalar.activation(s[:], a[:].rearrange("p t j -> p j t"), SILU)
+            s = pool.tile([P, TILE, PACK], F32, name=name, align_bytes=64)
+            nc.scalar.activation(s[:], a.rearrange("p t j -> p j t"), SILU)
             return s
 
         def product_on_vector(tile, s, h, bank):
-            b = psum.tile([P, PACK, TILE], F32, name="bank%d" % bank)
+            b = banks[bank][:].rearrange("p (t j) -> p t j", t=PACK)
             first_layer_sums(b, w3_w, w3_s, tile)
-            nc.vector.tensor_tensor(h, b[:].rearrange("p t j -> p j t"), s[:], MULT)
+            nc.vector.tensor_tensor(h, b.rearrange("p t j -> p j t"), s[:], MULT)
 
-        def value(tile, bank):
-            b = psum.tile([P, PACK, TILE], F32, name="bank%d" % bank)
+        def value(tile, bank, u):
+            b = banks[bank][:].rearrange("p (t j) -> p t j", t=PACK)
             first_layer_sums(b, w3_w, w3_s, tile)
-            u = ring.tile([P, TILE, PACK], F32, name="u")
-            nc.scalar.copy(u[:], b[:].rearrange("p t j -> p j t"))
+            nc.scalar.copy(u, b.rearrange("p t j -> p j t"))
             return u
 
         def product_on_gpsimd(s, u, h):
-            nc.gpsimd.tensor_tensor(h, u[:], s[:], MULT)
+            nc.gpsimd.tensor_tensor(h, u, s[:], MULT)
 
         def quantise(first, count, h):
             cols = slice(first, first + count)
-            words = h_w[first // CHUNK][:, first % CHUNK : first % CHUNK + count]
             nc.vector.quantize_mx(
-                out=words.bitcast(FP8X4), scales=h_s[:, cols], in_=h[:].rearrange("p j t -> p (j t)")
+                out=h_w[:, cols].bitcast(FP8X4), scales=h_s[:, cols], in_=h.rearrange("p j t -> p (j t)")
             )
 
-        def second_layer(n, first, count, name, bank):
+        def second_layer(n, first, count, z, bank):
             cols = slice(first, first + count)
-            z = keep.tile([P, count], F32, name=name, align_bytes=64)
-            o = psum.tile([P, count], F32, name="bank%d" % bank)
+            o = banks[bank][:, 0:count]
             nc.tensor.matmul_mx(
-                out=o[:],
+                out=o,
                 lhsT=w2_w[:, n * P : (n + 1) * P].bitcast(FP8X4),
                 lhsT_scale=ws[:, N + n * P : N + (n + 1) * P],
-                rhs=h_w[first // CHUNK][:].bitcast(FP8X4),
+                rhs=h_w[:, cols].bitcast(FP8X4),
                 rhs_scale=h_s[:, cols],
                 start=True,
                 stop=True,
             )
-            nc.scalar.copy(z[:], o[:])
+            nc.scalar.copy(z, o)
             return z
 
         def scatter(n, first, count, z):
-            nc.vector.tensor_copy(result[n][:].indirect(offset_columns(first, count)), z[:])
+            nc.vector.tensor_copy(result[n][:].indirect(offset_columns(first, count)), z)
 
-        def h_tile(name, tiles=1):
-            return keep.tile([P, tiles * TILE, PACK], BF16, name=name, align_bytes=64)
+        def z_tile(name):
+            z = keep.tile([P, CHUNK], F32, name=name, align_bytes=64)
+            return z[:]
+
+        def flat(tile, first):
+            return tile[:].rearrange("p j t -> p (j t)")[:, first : first + CHUNK]
 
         nc.vector.tensor_copy(g_s[:], x_s[:].indirect(offsets[:]))
         g0 = keep.tile([P, CHUNK], U32, name="g0", align_bytes=64)
@@ -204,57 +207,56 @@ def tile_moe_cas_glu_silu_kernel(
         light_layer(1, 0, 1)
         s0 = gate(0, 4)
         s1 = gate(1, 5)
-        s2 = gate(2, 0)
+        s2 = gate(2, 0, keep, "s2")
         s3 = gate(3, 6)
-        h_w = [keep.tile([P, CHUNK], U32, name="h_w%d" % c, align_bytes=64) for c in range(4)]
-        h = [h_tile("h%d" % tile) for tile in range(4)]
-        product_on_vector(0, s0, h[0][:], 2)
-        product_on_vector(1, s1, h[1][:], 3)
+        h_even = keep.tile([P, TILE, PACK], BF16, name="h_even", align_bytes=64)
+        h_pair = keep.tile([P, CHUNK, PACK], BF16, name="h_pair", align_bytes=64)
+        h = [h_even[:], h_pair[:, 0:TILE, :], h_even[:], h_pair[:, 0:TILE, :]]
+        product_on_vector(0, s0, h[0], 2)
+        product_on_vector(1, s1, h[1], 3)
         quantise(0, TILE, h[0])
         quantise(TILE, TILE, h[1])
-        product_on_vector(2, s2, h[2][:], 7)
-        product_on_vector(3, s3, h[3][:], 1)
-        z00 = second_layer(0, 0, CHUNK, "z00", 0)
+        product_on_vector(2, s2, h[2], 7)
+        product_on_vector(3, s3, h[3], 1)
+        z00 = second_layer(0, 0, CHUNK, flat(s2, 0), 0)
         light_layer(1, 1, 4)
         light_layer(1, 2, 5)
+        s4 = gate(4, 7)
         light_layer(1, 3, 1)
         quantise(2 * TILE, TILE, h[2])
         quantise(3 * TILE, TILE, h[3])
         scatter(0, 0, CHUNK, z00)
-        z10 = second_layer(1, 0, CHUNK, "z10", 6)
-        s4 = gate(4, 7)
-        u4 = value(4, 0)
-        h4 = h_tile("z00")
-        product_on_gpsimd(s4, u4, h4[:])
+        z10 = second_layer(1, 0, CHUNK, z_tile("z10"), 6)
         scatter(1, 0, CHUNK, z10)
-        quantise(4 * TILE, TILE, h4)
-        s5 = gate(5, 6)
-        u5 = value(5, 1)
-        z01 = second_layer(0, CHUNK, CHUNK, "z01", 0)
-        h5 = h_tile("z00")
-        product_on_gpsimd(s5, u5, h5[:])
+        h45 = h_pair
+        u45 = keep.tile([P, CHUNK, PACK], F32, name="u45", align_bytes=64)
+        u4 = value(4, 0, u45[:, 0:TILE, :])
+        product_on_gpsimd(s4, u4, h45[:, 0:TILE, :])
+        z01 = second_layer(0, CHUNK, CHUNK, z_tile("z01"), 1)
         scatter(0, CHUNK, CHUNK, z01)
-        quantise(5 * TILE, TILE, h5)
-        s6 = gate(6, 7)
-        u6 = value(6, 6)
-        z11 = second_layer(1, CHUNK, CHUNK, "z11", 1)
-        h6 = h_tile("z00")
-        product_on_gpsimd(s6, u6, h6[:])
+        s5 = gate(5, 7)
+        u5 = value(5, 6, u45[:, TILE:CHUNK, :])
+        product_on_gpsimd(s5, u5, h45[:, TILE : 2 * TILE, :])
+        quantise(4 * TILE, CHUNK, h45[:])
+        h67 = h_pair
+        s6 = gate(6, 0)
+        u67 = keep.tile([P, CHUNK, PACK], F32, name="u67", align_bytes=64)
+        u6 = value(6, 7, u67[:, 0:TILE, :])
+        product_on_gpsimd(s6, u6, h67[:, 0:TILE, :])
+        z11 = second_layer(1, CHUNK, CHUNK, flat(u45, 384), 0)
         scatter(1, CHUNK, CHUNK, z11)
-        quantise(6 * TILE, TILE, h6)
         s7 = gate(7, 0)
-        u7 = value(7, 7)
-        z02 = second_layer(0, 2 * CHUNK, CHUNK, "z02", 4)
-        h7 = h_tile("z00")
-        product_on_gpsimd(s7, u7, h7[:])
+        u7 = value(7, 1, u67[:, TILE:CHUNK, :])
+        product_on_gpsimd(s7, u7, h67[:, TILE : 2 * TILE, :])
+        z02 = second_layer(0, 2 * CHUNK, CHUNK, z_tile("z02"), 4)
         scatter(0, 2 * CHUNK, CHUNK, z02)
-        quantise(7 * TILE, TILE, h7)
-        z12 = second_layer(1, 2 * CHUNK, CHUNK, "z12", 4)
+        quantise(6 * TILE, CHUNK, h67[:])
+        z12 = second_layer(1, 2 * CHUNK, CHUNK, flat(u67, 384), 5)
         scatter(1, 2 * CHUNK, CHUNK, z12)
-        z03 = second_layer(0, 3 * CHUNK, CHUNK, "z03", 5)
+        z03 = second_layer(0, 3 * CHUNK, CHUNK, z_tile("z03"), 4)
         scatter(0, 3 * CHUNK, CHUNK, z03)
         nc.sync.dma_start(out=out[0:P, :], in_=result[0][:])
-        z13 = second_layer(1, 3 * CHUNK, CHUNK, "z13", 4)
+        z13 = second_layer(1, 3 * CHUNK, CHUNK, z_tile("z13"), 2)
         scatter(1, 3 * CHUNK, CHUNK, z13)
         nc.sync.dma_start(out=out[P : 2 * P, 0 : T // 2], in_=result[1][:, 0 : T // 2])
         nc.scalar.dma_start(out=out[P : 2 * P, T // 2 : T], in_=result[1][:, T // 2 : T])

@@ -43,7 +43,6 @@ def tile_moe_cas_glu_silu_kernel(
     nc = tc.nc
     with ExitStack() as ctx:
         keep = ctx.enter_context(tc.tile_pool(name="keep", bufs=1))
-        ring = ctx.enter_context(tc.tile_pool(name="ring", bufs=6))
         psum = ctx.enter_context(tc.psum_pool(name="psum", bufs=1))
 
         offsets = keep.tile([P, S // PER_COLUMN], U16, name="offsets")
@@ -106,23 +105,19 @@ def tile_moe_cas_glu_silu_kernel(
                 plane[:].rearrange("p (t m) -> p t m", t=PACK), raw.rearrange("p (m t) -> p t m", t=PACK)
             )
 
-        def light_layer(n, b, bank, on_vector=False):
-            if True:
-                cols = slice(b * BANK, (b + 1) * BANK)
-                y = banks[bank]
-                nc.tensor.matmul_mx(
-                    out=y[:],
-                    lhsT=w_w[:, n * P : (n + 1) * P].bitcast(FP8X4),
-                    lhsT_scale=ws[:, n * P : (n + 1) * P],
-                    rhs=x_w[:, cols].bitcast(FP8X4),
-                    rhs_scale=x_s[:, cols],
-                    start=True,
-                    stop=True,
-                )
-                if on_vector:
-                    nc.vector.tensor_copy(result[n][:, cols], y[:])
-                else:
-                    nc.scalar.copy(result[n][:, cols], y[:])
+        def light_layer(n, b, bank):
+            cols = slice(b * BANK, (b + 1) * BANK)
+            y = banks[bank]
+            nc.tensor.matmul_mx(
+                out=y[:],
+                lhsT=w_w[:, n * P : (n + 1) * P].bitcast(FP8X4),
+                lhsT_scale=ws[:, n * P : (n + 1) * P],
+                rhs=x_w[:, cols].bitcast(FP8X4),
+                rhs_scale=x_s[:, cols],
+                start=True,
+                stop=True,
+            )
+            nc.scalar.copy(result[n][:, cols], y[:])
 
         def first_layer_sums(bank, words, plane, tile):
             for t in range(PACK):
@@ -136,17 +131,16 @@ def tile_moe_cas_glu_silu_kernel(
                     stop=True,
                 )
 
-        def gate(tile, bank, pool=ring, name="s"):
+        def gate(tile, bank, s):
             a = banks[bank][:].rearrange("p (t j) -> p t j", t=PACK)
             first_layer_sums(a, w1_w, w1_s, tile)
-            s = pool.tile([P, TILE, PACK], F32, name=name, align_bytes=64)
-            nc.scalar.activation(s[:], a.rearrange("p t j -> p j t"), SILU)
+            nc.scalar.activation(s, a.rearrange("p t j -> p j t"), SILU)
             return s
 
         def product_on_vector(tile, s, h, bank):
             b = banks[bank][:].rearrange("p (t j) -> p t j", t=PACK)
             first_layer_sums(b, w3_w, w3_s, tile)
-            nc.vector.tensor_tensor(h, b.rearrange("p t j -> p j t"), s[:], MULT)
+            nc.vector.tensor_tensor(h, b.rearrange("p t j -> p j t"), s, MULT)
 
         def value(tile, bank, u):
             b = banks[bank][:].rearrange("p (t j) -> p t j", t=PACK)
@@ -155,7 +149,7 @@ def tile_moe_cas_glu_silu_kernel(
             return u
 
         def product_on_gpsimd(s, u, h):
-            nc.gpsimd.tensor_tensor(h, u, s[:], MULT)
+            nc.gpsimd.tensor_tensor(h, u, s, MULT)
 
         def quantise(first, count, h):
             cols = slice(first, first + count)
@@ -164,18 +158,19 @@ def tile_moe_cas_glu_silu_kernel(
             )
 
         def second_layer(n, first, count, z, bank):
-            cols = slice(first, first + count)
-            o = banks[bank][:, 0:count]
-            nc.tensor.matmul_mx(
-                out=o,
-                lhsT=w2_w[:, n * P : (n + 1) * P].bitcast(FP8X4),
-                lhsT_scale=ws[:, N + n * P : N + (n + 1) * P],
-                rhs=h_w[:, cols].bitcast(FP8X4),
-                rhs_scale=h_s[:, cols],
-                start=True,
-                stop=True,
-            )
-            nc.scalar.copy(z, o)
+            for done in range(0, count, CHUNK):
+                width = min(CHUNK, count - done)
+                cols = slice(first + done, first + done + width)
+                nc.tensor.matmul_mx(
+                    out=banks[bank][:, done : done + width],
+                    lhsT=w2_w[:, n * P : (n + 1) * P].bitcast(FP8X4),
+                    lhsT_scale=ws[:, N + n * P : N + (n + 1) * P],
+                    rhs=h_w[:, cols].bitcast(FP8X4),
+                    rhs_scale=h_s[:, cols],
+                    start=True,
+                    stop=True,
+                )
+            nc.scalar.copy(z, banks[bank][:, 0:count])
             return z
 
         def scatter(n, first, count, z):
@@ -185,8 +180,8 @@ def tile_moe_cas_glu_silu_kernel(
             z = keep.tile([P, CHUNK], F32, name=name, align_bytes=64)
             return z[:]
 
-        def flat(tile, first):
-            return tile[:].rearrange("p j t -> p (j t)")[:, first : first + CHUNK]
+        def tokens(tile, first):
+            return tile[:, first : first + BANK].rearrange("p (j t) -> p j t", t=PACK)
 
         nc.vector.tensor_copy(g_s[:], x_s[:].indirect(offsets[:]))
         g0 = keep.tile([P, CHUNK], U32, name="g0", align_bytes=64)
@@ -202,61 +197,60 @@ def tile_moe_cas_glu_silu_kernel(
         gather_words(g23[:, CHUNK : 2 * CHUNK], 3)
         g_w = [g[:, j * TILE : (j + 1) * TILE] for g, k in ((g0, 2), (g1, 2), (g23, 4)) for j in range(k)]
 
+        early = keep.tile([P, 5 * BANK], F32, name="early", align_bytes=64)
+        late_s = keep.tile([P, 11 * TILE], F32, name="late_s", align_bytes=64)
+        late_u = keep.tile([P, 2 * BANK], F32, name="late_u", align_bytes=64)
+        h_even = keep.tile([P, TILE, PACK], BF16, name="h_even", align_bytes=64)
+        h_pair = keep.tile([P, CHUNK, PACK], BF16, name="h_pair", align_bytes=64)
+        h_a = h_pair[:, 0:TILE, :]
+        h_b = h_pair[:, TILE:CHUNK, :]
         for b in range(4):
             light_layer(0, b, b)
         light_layer(1, 0, 1)
-        s0 = gate(0, 4)
-        s1 = gate(1, 5)
-        s2 = gate(2, 0, keep, "s2")
-        s3 = gate(3, 6)
-        h_even = keep.tile([P, TILE, PACK], BF16, name="h_even", align_bytes=64)
-        h_pair = keep.tile([P, CHUNK, PACK], BF16, name="h_pair", align_bytes=64)
-        h = [h_even[:], h_pair[:, 0:TILE, :], h_even[:], h_pair[:, 0:TILE, :]]
-        product_on_vector(0, s0, h[0], 2)
-        product_on_vector(1, s1, h[1], 3)
-        quantise(0, TILE, h[0])
-        quantise(TILE, TILE, h[1])
-        product_on_vector(2, s2, h[2], 7)
-        product_on_vector(3, s3, h[3], 1)
-        z00 = second_layer(0, 0, CHUNK, flat(s2, 0), 0)
-        light_layer(1, 1, 4)
-        light_layer(1, 2, 5)
-        s4 = gate(4, 7)
-        light_layer(1, 3, 1)
-        quantise(2 * TILE, TILE, h[2])
-        quantise(3 * TILE, TILE, h[3])
+        s0 = gate(0, 4, tokens(early, 0))
+        s1 = gate(1, 5, tokens(early, BANK))
+        s2 = gate(2, 0, tokens(early, 2 * BANK))
+        s3 = gate(3, 6, tokens(late_s, 7 * TILE // 2))
+        product_on_vector(0, s0, h_even[:], 2)
+        product_on_vector(1, s1, h_a, 3)
+        quantise(0, TILE, h_even[:])
+        quantise(TILE, TILE, h_a)
+        product_on_vector(2, s2, h_even[:], 7)
+        product_on_vector(3, s3, h_a, 1)
+        quantise(2 * TILE, TILE, h_even[:])
+        quantise(3 * TILE, TILE, h_a)
+        s4 = gate(4, 4, tokens(early, 3 * BANK))
+        u4 = value(4, 5, tokens(early, 4 * BANK))
+        product_on_gpsimd(s4, u4, h_a)
+        z00 = second_layer(0, 0, CHUNK, z_tile("z00"), 2)
         scatter(0, 0, CHUNK, z00)
-        z10 = second_layer(1, 0, CHUNK, z_tile("z10"), 6)
-        scatter(1, 0, CHUNK, z10)
-        h45 = h_pair
-        u45 = keep.tile([P, CHUNK, PACK], F32, name="u45", align_bytes=64)
-        u4 = value(4, 0, u45[:, 0:TILE, :])
-        product_on_gpsimd(s4, u4, h45[:, 0:TILE, :])
-        z01 = second_layer(0, CHUNK, CHUNK, z_tile("z01"), 1)
+        s5 = gate(5, 0, tokens(late_s, 7 * TILE // 2))
+        u5 = value(5, 1, tokens(late_u, CHUNK))
+        product_on_gpsimd(s5, u5, h_b)
+        z01 = second_layer(0, CHUNK, CHUNK, z_tile("z01"), 3)
         scatter(0, CHUNK, CHUNK, z01)
-        s5 = gate(5, 7)
-        u5 = value(5, 6, u45[:, TILE:CHUNK, :])
-        product_on_gpsimd(s5, u5, h45[:, TILE : 2 * TILE, :])
-        quantise(4 * TILE, CHUNK, h45[:])
-        h67 = h_pair
-        s6 = gate(6, 0)
-        u67 = keep.tile([P, CHUNK, PACK], F32, name="u67", align_bytes=64)
-        u6 = value(6, 7, u67[:, 0:TILE, :])
-        product_on_gpsimd(s6, u6, h67[:, 0:TILE, :])
-        z11 = second_layer(1, CHUNK, CHUNK, flat(u45, 384), 0)
-        scatter(1, CHUNK, CHUNK, z11)
-        s7 = gate(7, 0)
-        u7 = value(7, 1, u67[:, TILE:CHUNK, :])
-        product_on_gpsimd(s7, u7, h67[:, TILE : 2 * TILE, :])
-        z02 = second_layer(0, 2 * CHUNK, CHUNK, z_tile("z02"), 4)
+        quantise(4 * TILE, CHUNK, h_pair[:])
+        light_layer(1, 1, 7)
+        light_layer(1, 2, 2)
+        light_layer(1, 3, 0)
+        z10 = second_layer(1, 0, 3 * TILE, late_s[:, 4 * TILE : 7 * TILE], 4)
+        scatter(1, 0, 3 * TILE, z10)
+        s6 = gate(6, 5, tokens(late_s, 0))
+        u6 = value(6, 1, tokens(late_u, 0))
+        product_on_gpsimd(s6, u6, h_a)
+        s7 = gate(7, 7, tokens(late_s, 7 * TILE))
+        z02 = second_layer(0, 2 * CHUNK, CHUNK, z_tile("z02"), 6)
         scatter(0, 2 * CHUNK, CHUNK, z02)
-        quantise(6 * TILE, CHUNK, h67[:])
-        z12 = second_layer(1, 2 * CHUNK, CHUNK, flat(u67, 384), 5)
-        scatter(1, 2 * CHUNK, CHUNK, z12)
-        z03 = second_layer(0, 3 * CHUNK, CHUNK, z_tile("z03"), 4)
+        u7 = value(7, 2, tokens(late_u, BANK))
+        product_on_gpsimd(s7, u7, h_b)
+        quantise(6 * TILE, CHUNK, h_pair[:])
+        z11 = second_layer(1, 3 * TILE, CHUNK, late_u[:, BANK : BANK + CHUNK], 3)
+        scatter(1, 3 * TILE, CHUNK, z11)
+        z03 = second_layer(0, 3 * CHUNK, CHUNK, z_tile("z03"), 0)
         scatter(0, 3 * CHUNK, CHUNK, z03)
         nc.sync.dma_start(out=out[0:P, :], in_=result[0][:])
-        z13 = second_layer(1, 3 * CHUNK, CHUNK, z_tile("z13"), 2)
-        scatter(1, 3 * CHUNK, CHUNK, z13)
+        z12 = keep.tile([P, 3 * TILE], F32, name="z12", align_bytes=64)
+        second_layer(1, 5 * TILE, 3 * TILE, z12[:], 4)
+        scatter(1, 5 * TILE, 3 * TILE, z12[:])
         nc.sync.dma_start(out=out[P : 2 * P, 0 : T // 2], in_=result[1][:, 0 : T // 2])
         nc.scalar.dma_start(out=out[P : 2 * P, T // 2 : T], in_=result[1][:, T // 2 : T])

@@ -21,6 +21,7 @@ BANK = 512
 TILE = 128
 CHUNK = 256
 PER_COLUMN = 16
+XA = 1024
 
 
 def load_words(queue, tile, words):
@@ -77,10 +78,10 @@ def tile_moe_cas_glu_silu_kernel(
         load_words(nc.sync, w_w[:], w_words)
         load_scales(nc.sync, x_s, 0, 0, x_scales)
         load_scales(nc.sync, ws, 0, 0, w_scales, range(0, 1))
-        nc.sync.dma_start(out=x_w[:, 0 : T // 2], in_=x_dram[:, 0 : T // 2])
+        nc.sync.dma_start(out=x_w[:, 0 : XA], in_=x_dram[:, 0 : XA])
         load_scales(nc.sync, ws, 0, 0, w_scales, range(1, 4))
-        nc.sync.dma_start(out=x_w[:, T // 2 : T], in_=x_dram[:, T // 2 : T])
         load_words(nc.sync, w1_raw[:], w1_words)
+        nc.sync.dma_start(out=x_w[:, XA : T], in_=x_dram[:, XA : T])
         load_scales(nc.sync, ws, 0, 2 * N, w1_scales)
         load_words(nc.sync, w3_raw[:], w3_words)
         load_scales(nc.sync, w3s_raw, 0, 0, w3_scales, range(0, 1))
@@ -184,67 +185,69 @@ def tile_moe_cas_glu_silu_kernel(
             return tile[:, first : first + BANK].rearrange("p (j t) -> p j t", t=PACK)
 
         nc.vector.tensor_copy(g_s[:], x_s[:].indirect(offsets[:]))
+        permute_words(nc.vector, w1_w, w1_raw[:])
         g0 = keep.tile([P, CHUNK], U32, name="g0", align_bytes=64)
         gather_words(g0[:], 0)
-        permute_words(nc.vector, w1_w, w1_raw[:])
         permute_scales(nc.gpsimd, w1_s, ws[:, 2 * N : 2 * N + H])
-        g1 = keep.tile([P, CHUNK], U32, name="w1_raw", align_bytes=64)
-        gather_words(g1[:], 1)
+        g1 = keep.tile([P, CHUNK], U32, name="g3", align_bytes=64)
+        gather_words(g1[:], 3)
         permute_words(nc.gpsimd, w3_w, w3_raw[:])
         permute_scales(nc.vector, w3_s, w3s_raw[:])
         g23 = keep.tile([P, 2 * CHUNK], U32, name="stage", align_bytes=64)
-        gather_words(g23[:, 0:CHUNK], 2)
-        gather_words(g23[:, CHUNK : 2 * CHUNK], 3)
-        g_w = [g[:, j * TILE : (j + 1) * TILE] for g, k in ((g0, 2), (g1, 2), (g23, 4)) for j in range(k)]
+        gather_words(g23[:, 0:CHUNK], 1)
+        gather_words(g23[:, CHUNK : 2 * CHUNK], 2)
+        g_w = [g[:, j * TILE : (j + 1) * TILE] for g, k in ((g0, 2), (g23, 4), (g1, 2)) for j in range(k)]
 
-        early = keep.tile([P, 5 * BANK], F32, name="early", align_bytes=64)
+        early = keep.tile([P, 4 * BANK], F32, name="early", align_bytes=64)
         late_s = keep.tile([P, 11 * TILE], F32, name="late_s", align_bytes=64)
         late_u = keep.tile([P, 2 * BANK], F32, name="late_u", align_bytes=64)
         h_even = keep.tile([P, TILE, PACK], BF16, name="h_even", align_bytes=64)
         h_pair = keep.tile([P, CHUNK, PACK], BF16, name="h_pair", align_bytes=64)
         h_a = h_pair[:, 0:TILE, :]
         h_b = h_pair[:, TILE:CHUNK, :]
-        for b in range(4):
-            light_layer(0, b, b)
-        light_layer(1, 0, 1)
+        light_layer(0, 0, 0)
+        light_layer(0, 1, 1)
+        light_layer(1, 0, 7)
+        light_layer(0, 2, 2)
+        light_layer(0, 3, 3)
         s0 = gate(0, 4, tokens(early, 0))
         s1 = gate(1, 5, tokens(early, BANK))
-        s2 = gate(2, 0, tokens(early, 2 * BANK))
-        s3 = gate(3, 6, tokens(late_s, 7 * TILE // 2))
         product_on_vector(0, s0, h_even[:], 2)
         product_on_vector(1, s1, h_a, 3)
+        s2 = gate(2, 0, tokens(late_u, CHUNK))
+        s3 = gate(3, 6, tokens(late_s, 7 * TILE // 2))
         quantise(0, TILE, h_even[:])
         quantise(TILE, TILE, h_a)
         product_on_vector(2, s2, h_even[:], 7)
         product_on_vector(3, s3, h_a, 1)
         quantise(2 * TILE, TILE, h_even[:])
         quantise(3 * TILE, TILE, h_a)
-        s4 = gate(4, 4, tokens(early, 3 * BANK))
-        u4 = value(4, 5, tokens(early, 4 * BANK))
+        s4 = gate(4, 4, tokens(early, 2 * BANK))
+        u4 = value(4, 5, tokens(early, 3 * BANK))
         product_on_gpsimd(s4, u4, h_a)
         z00 = second_layer(0, 0, CHUNK, z_tile("z00"), 2)
         scatter(0, 0, CHUNK, z00)
         s5 = gate(5, 0, tokens(late_s, 7 * TILE // 2))
-        u5 = value(5, 1, tokens(late_u, CHUNK))
+        u5 = value(5, 6, tokens(late_u, CHUNK))
         product_on_gpsimd(s5, u5, h_b)
         z01 = second_layer(0, CHUNK, CHUNK, z_tile("z01"), 3)
         scatter(0, CHUNK, CHUNK, z01)
         quantise(4 * TILE, CHUNK, h_pair[:])
         light_layer(1, 1, 7)
-        light_layer(1, 2, 2)
+        light_layer(1, 2, 6)
         light_layer(1, 3, 0)
         z10 = second_layer(1, 0, 3 * TILE, late_s[:, 4 * TILE : 7 * TILE], 4)
         scatter(1, 0, 3 * TILE, z10)
         s6 = gate(6, 5, tokens(late_s, 0))
-        u6 = value(6, 1, tokens(late_u, 0))
+        u6 = value(6, 3, tokens(late_u, 0))
         product_on_gpsimd(s6, u6, h_a)
         s7 = gate(7, 7, tokens(late_s, 7 * TILE))
-        z02 = second_layer(0, 2 * CHUNK, CHUNK, z_tile("z02"), 6)
+        z02 = second_layer(0, 2 * CHUNK, CHUNK, z_tile("z02"), 2)
         scatter(0, 2 * CHUNK, CHUNK, z02)
-        u7 = value(7, 2, tokens(late_u, BANK))
+        u7 = value(7, 6, tokens(late_u, BANK))
         product_on_gpsimd(s7, u7, h_b)
         quantise(6 * TILE, CHUNK, h_pair[:])
-        z11 = second_layer(1, 3 * TILE, CHUNK, late_u[:, BANK : BANK + CHUNK], 3)
+        z11 = second_layer(1, 3 * TILE, CHUNK, late_u[:, BANK : BANK + CHUNK], 1)
         scatter(1, 3 * TILE, CHUNK, z11)
         z03 = second_layer(0, 3 * CHUNK, CHUNK, z_tile("z03"), 0)
         scatter(0, 3 * CHUNK, CHUNK, z03)

@@ -21,7 +21,8 @@ BANK = 512
 TILE = 128
 CHUNK = 256
 PER_COLUMN = 16
-XA = 1024
+XA = 1280
+VECTOR_CLEARS = 1344
 
 
 def load_words(queue, tile, words):
@@ -65,27 +66,28 @@ def tile_moe_cas_glu_silu_kernel(
         banks = [psum.tile([P, BANK], F32, name="bank%d" % b) for b in range(8)]
         result = [keep.tile([P, T], F32, name="result%d" % n) for n in range(N // P)]
 
-        nc.vector.memset(x_s[:, 0 : T // 2].bitcast(I32), 0)
-        nc.gpsimd.memset(x_s[:, T // 2 : T].bitcast(I32), 0)
+        nc.vector.memset(x_s[:, 0:VECTOR_CLEARS].bitcast(I32), 0)
+        nc.gpsimd.memset(x_s[:, VECTOR_CLEARS:T].bitcast(I32), 0)
         nc.vector.memset(ws[:].bitcast(I32), 0)
         nc.vector.memset(w3s_raw[:].bitcast(I32), 0)
         warm = keep.tile([P, 2], F32, name="warm")
-        nc.gpsimd.memset(warm[:, 0:1], 0.0)
-        nc.scalar.activation(warm[:, 1:2], warm[:, 0:1], SILU)
+        nc.vector.memset(warm[:, 0:1], 0.0)
 
         x_dram = x_words[0].rearrange("p n d -> p (n d)").bitcast(I32)
+        nc.scalar.activation(warm[:, 1:2], warm[:, 0:1], SILU)
         nc.sync.dma_start(offsets[:], offs)
         load_words(nc.sync, w_w[:], w_words)
         load_scales(nc.sync, x_s, 0, 0, x_scales)
         load_scales(nc.sync, ws, 0, 0, w_scales, range(0, 1))
-        nc.sync.dma_start(out=x_w[:, 0 : XA], in_=x_dram[:, 0 : XA])
+        nc.sync.dma_start(out=x_w[:, 0:XA], in_=x_dram[:, 0:XA])
         load_scales(nc.sync, ws, 0, 0, w_scales, range(1, 4))
+        nc.sync.dma_start(out=x_w[:, XA:T], in_=x_dram[:, XA:T])
         load_words(nc.sync, w1_raw[:], w1_words)
-        nc.sync.dma_start(out=x_w[:, XA : T], in_=x_dram[:, XA : T])
-        load_scales(nc.sync, ws, 0, 2 * N, w1_scales)
+        load_scales(nc.sync, ws, 0, 2 * N, w1_scales, range(0, 2))
+        load_scales(nc.gpsimd, ws, 0, 2 * N, w1_scales, range(2, 4))
         load_words(nc.sync, w3_raw[:], w3_words)
-        load_scales(nc.sync, w3s_raw, 0, 0, w3_scales, range(0, 1))
-        load_scales(nc.gpsimd, w3s_raw, 0, 0, w3_scales, range(1, 4))
+        load_scales(nc.gpsimd, w3s_raw, 0, 0, w3_scales, range(3, 4))
+        load_scales(nc.sync, w3s_raw, 0, 0, w3_scales, range(0, 3))
         load_scales(nc.sync, ws, 0, N, w2_scales)
         load_words(nc.sync, w2_w[:], w2_words)
 
@@ -106,11 +108,11 @@ def tile_moe_cas_glu_silu_kernel(
                 plane[:].rearrange("p (t m) -> p t m", t=PACK), raw.rearrange("p (m t) -> p t m", t=PACK)
             )
 
-        def light_layer(n, b, bank):
-            cols = slice(b * BANK, (b + 1) * BANK)
-            y = banks[bank]
+        def light_layer(n, first, count, bank):
+            cols = slice(first, first + count)
+            y = banks[bank][:, 0:count]
             nc.tensor.matmul_mx(
-                out=y[:],
+                out=y,
                 lhsT=w_w[:, n * P : (n + 1) * P].bitcast(FP8X4),
                 lhsT_scale=ws[:, n * P : (n + 1) * P],
                 rhs=x_w[:, cols].bitcast(FP8X4),
@@ -118,7 +120,7 @@ def tile_moe_cas_glu_silu_kernel(
                 start=True,
                 stop=True,
             )
-            nc.scalar.copy(result[n][:, cols], y[:])
+            nc.scalar.copy(result[n][:, cols], y)
 
         def first_layer_sums(bank, words, plane, tile):
             for t in range(PACK):
@@ -189,71 +191,81 @@ def tile_moe_cas_glu_silu_kernel(
         g0 = keep.tile([P, CHUNK], U32, name="g0", align_bytes=64)
         gather_words(g0[:], 0)
         permute_scales(nc.gpsimd, w1_s, ws[:, 2 * N : 2 * N + H])
-        g1 = keep.tile([P, CHUNK], U32, name="g3", align_bytes=64)
-        gather_words(g1[:], 3)
+        g1 = keep.tile([P, CHUNK], U32, name="g1", align_bytes=64)
+        gather_words(g1[:], 1)
         permute_words(nc.gpsimd, w3_w, w3_raw[:])
         permute_scales(nc.vector, w3_s, w3s_raw[:])
         g23 = keep.tile([P, 2 * CHUNK], U32, name="stage", align_bytes=64)
-        gather_words(g23[:, 0:CHUNK], 1)
-        gather_words(g23[:, CHUNK : 2 * CHUNK], 2)
-        g_w = [g[:, j * TILE : (j + 1) * TILE] for g, k in ((g0, 2), (g23, 4), (g1, 2)) for j in range(k)]
+        gather_words(g23[:, 0:CHUNK], 2)
+        gather_words(g23[:, CHUNK : 2 * CHUNK], 3)
+        g_w = [g[:, j * TILE : (j + 1) * TILE] for g, k in ((g0, 2), (g1, 2), (g23, 4)) for j in range(k)]
 
-        early = keep.tile([P, 4 * BANK], F32, name="early", align_bytes=64)
-        late_s = keep.tile([P, 11 * TILE], F32, name="late_s", align_bytes=64)
-        late_u = keep.tile([P, 2 * BANK], F32, name="late_u", align_bytes=64)
+        early = keep.tile([P, 6 * BANK], F32, name="early", align_bytes=64)
+        late = keep.tile([P, 15 * TILE], F32, name="late", align_bytes=64)
         h_even = keep.tile([P, TILE, PACK], BF16, name="h_even", align_bytes=64)
         h_pair = keep.tile([P, CHUNK, PACK], BF16, name="h_pair", align_bytes=64)
         h_a = h_pair[:, 0:TILE, :]
         h_b = h_pair[:, TILE:CHUNK, :]
-        light_layer(0, 0, 0)
-        light_layer(0, 1, 1)
-        light_layer(1, 0, 7)
-        light_layer(0, 2, 2)
-        light_layer(0, 3, 3)
+        for r in range(5):
+            nc.tensor.matmul_mx(
+                out=banks[5][:, 0:CHUNK],
+                lhsT=w_w[:, 0:P].bitcast(FP8X4),
+                lhsT_scale=x_s[:, 0:P],
+                rhs=w_w[:].bitcast(FP8X4),
+                rhs_scale=x_s[:, 0:CHUNK],
+                start=True,
+                stop=True,
+            )
+        for piece, bank in enumerate((0, 7, 6, 2)):
+            light_layer(0, piece * CHUNK, CHUNK, bank)
+        light_layer(0, 2 * BANK, BANK, 1)
+        light_layer(0, 3 * BANK, BANK, 3)
+        light_layer(1, 0, CHUNK, 0)
         s0 = gate(0, 4, tokens(early, 0))
         s1 = gate(1, 5, tokens(early, BANK))
+        s2 = gate(2, 7, tokens(early, 4 * BANK))
+        s3 = gate(3, 6, tokens(late, 11 * TILE // 2))
         product_on_vector(0, s0, h_even[:], 2)
-        product_on_vector(1, s1, h_a, 3)
-        s2 = gate(2, 0, tokens(late_u, CHUNK))
-        s3 = gate(3, 6, tokens(late_s, 7 * TILE // 2))
+        product_on_vector(1, s1, h_a, 1)
         quantise(0, TILE, h_even[:])
         quantise(TILE, TILE, h_a)
-        product_on_vector(2, s2, h_even[:], 7)
-        product_on_vector(3, s3, h_a, 1)
+        product_on_vector(2, s2, h_even[:], 3)
+        product_on_vector(3, s3, h_a, 0)
         quantise(2 * TILE, TILE, h_even[:])
         quantise(3 * TILE, TILE, h_a)
         s4 = gate(4, 4, tokens(early, 2 * BANK))
         u4 = value(4, 5, tokens(early, 3 * BANK))
         product_on_gpsimd(s4, u4, h_a)
+        light_layer(1, CHUNK, CHUNK, 6)
         z00 = second_layer(0, 0, CHUNK, z_tile("z00"), 2)
         scatter(0, 0, CHUNK, z00)
-        s5 = gate(5, 0, tokens(late_s, 7 * TILE // 2))
-        u5 = value(5, 6, tokens(late_u, CHUNK))
+        s5 = gate(5, 7, tokens(late, 7 * TILE // 2))
+        u5 = value(5, 3, tokens(late, 15 * TILE // 2))
         product_on_gpsimd(s5, u5, h_b)
-        z01 = second_layer(0, CHUNK, CHUNK, z_tile("z01"), 3)
+        z01 = second_layer(0, CHUNK, CHUNK, z_tile("z01"), 4)
         scatter(0, CHUNK, CHUNK, z01)
         quantise(4 * TILE, CHUNK, h_pair[:])
-        light_layer(1, 1, 7)
-        light_layer(1, 2, 6)
-        light_layer(1, 3, 0)
-        z10 = second_layer(1, 0, 3 * TILE, late_s[:, 4 * TILE : 7 * TILE], 4)
+        light_layer(1, BANK, BANK, 5)
+        light_layer(1, 2 * BANK, BANK, 0)
+        light_layer(1, 3 * BANK, BANK, 2)
+        z10 = second_layer(1, 0, 3 * TILE, late[:, 4 * TILE : 7 * TILE], 1)
         scatter(1, 0, 3 * TILE, z10)
-        s6 = gate(6, 5, tokens(late_s, 0))
-        u6 = value(6, 3, tokens(late_u, 0))
+        s6 = gate(6, 7, tokens(late, 0))
+        u6 = value(6, 3, tokens(late, 11 * TILE))
         product_on_gpsimd(s6, u6, h_a)
-        s7 = gate(7, 7, tokens(late_s, 7 * TILE))
-        z02 = second_layer(0, 2 * CHUNK, CHUNK, z_tile("z02"), 2)
+        s7 = gate(7, 4, tokens(late, 7 * TILE))
+        z02 = second_layer(0, 2 * CHUNK, CHUNK, z_tile("z02"), 6)
         scatter(0, 2 * CHUNK, CHUNK, z02)
-        u7 = value(7, 6, tokens(late_u, BANK))
+        u7 = value(7, 1, tokens(early, 5 * BANK))
         product_on_gpsimd(s7, u7, h_b)
         quantise(6 * TILE, CHUNK, h_pair[:])
-        z11 = second_layer(1, 3 * TILE, CHUNK, late_u[:, BANK : BANK + CHUNK], 1)
+        z11 = second_layer(1, 3 * TILE, CHUNK, early[:, 5 * BANK : 5 * BANK + CHUNK], 5)
         scatter(1, 3 * TILE, CHUNK, z11)
         z03 = second_layer(0, 3 * CHUNK, CHUNK, z_tile("z03"), 0)
         scatter(0, 3 * CHUNK, CHUNK, z03)
         nc.sync.dma_start(out=out[0:P, :], in_=result[0][:])
         z12 = keep.tile([P, 3 * TILE], F32, name="z12", align_bytes=64)
-        second_layer(1, 5 * TILE, 3 * TILE, z12[:], 4)
+        second_layer(1, 5 * TILE, 3 * TILE, z12[:], 2)
         scatter(1, 5 * TILE, 3 * TILE, z12[:])
         nc.sync.dma_start(out=out[P : 2 * P, 0 : T // 2], in_=result[1][:, 0 : T // 2])
         nc.scalar.dma_start(out=out[P : 2 * P, T // 2 : T], in_=result[1][:, T // 2 : T])

@@ -83,11 +83,10 @@ def tile_moe_cas_glu_silu_kernel(
         load_scales(nc.sync, ws, 0, 0, w_scales, range(1, 4))
         nc.sync.dma_start(out=x_w[:, XA:T], in_=x_dram[:, XA:T])
         load_words(nc.sync, w1_raw[:], w1_words)
-        load_scales(nc.sync, ws, 0, 2 * N, w1_scales, range(0, 2))
-        load_scales(nc.gpsimd, ws, 0, 2 * N, w1_scales, range(2, 4))
+        load_scales(nc.sync, ws, 0, 2 * N, w1_scales)
         load_words(nc.sync, w3_raw[:], w3_words)
-        load_scales(nc.gpsimd, w3s_raw, 0, 0, w3_scales, range(3, 4))
-        load_scales(nc.sync, w3s_raw, 0, 0, w3_scales, range(0, 3))
+        load_scales(nc.gpsimd, w3s_raw, 0, 0, w3_scales, range(2, 4))
+        load_scales(nc.sync, w3s_raw, 0, 0, w3_scales, range(0, 2))
         load_scales(nc.sync, ws, 0, N, w2_scales)
         load_words(nc.sync, w2_w[:], w2_words)
 
@@ -190,10 +189,10 @@ def tile_moe_cas_glu_silu_kernel(
         permute_words(nc.vector, w1_w, w1_raw[:])
         g0 = keep.tile([P, CHUNK], U32, name="g0", align_bytes=64)
         gather_words(g0[:], 0)
-        permute_scales(nc.gpsimd, w1_s, ws[:, 2 * N : 2 * N + H])
+        permute_scales(nc.vector, w1_s, ws[:, 2 * N : 2 * N + H])
         g1 = keep.tile([P, CHUNK], U32, name="g1", align_bytes=64)
         gather_words(g1[:], 1)
-        permute_words(nc.gpsimd, w3_w, w3_raw[:])
+        permute_words(nc.vector, w3_w, w3_raw[:])
         permute_scales(nc.vector, w3_s, w3s_raw[:])
         g23 = keep.tile([P, 2 * CHUNK], U32, name="stage", align_bytes=64)
         gather_words(g23[:, 0:CHUNK], 2)

@@ -22,7 +22,6 @@ TILE = 128
 CHUNK = 256
 PER_COLUMN = 16
 XA = 1280
-VECTOR_CLEARS = 1344
 
 
 def load_words(queue, tile, words):
@@ -53,11 +52,11 @@ def tile_moe_cas_glu_silu_kernel(
         w_w = keep.tile([P, N], I32, name="w_w", align_bytes=64)
         w2_w = keep.tile([P, N], I32, name="w2_w", align_bytes=64)
         w1_raw = keep.tile([P, H], I32, name="w1_raw", align_bytes=64)
-        w3_raw = keep.tile([P, H], I32, name="w3_raw", align_bytes=64)
+        w3_raw = keep.tile([P, H], I32, name="stage", align_bytes=64)
         w1_w = keep.tile([P, H], I32, name="w1_w", align_bytes=64)
         w3_w = keep.tile([P, H], I32, name="w3_w", align_bytes=64)
         ws = keep.tile([P, 2 * N + H], U8, name="ws", align_bytes=64)
-        w3s_raw = keep.tile([P, H], U8, name="stage", align_bytes=64)
+        w3s_raw = keep.tile([P, H], U8, name="w3s_raw", align_bytes=64)
         w1_s = keep.tile([P, H], U8, name="w1_s", align_bytes=64)
         w3_s = keep.tile([P, H], U8, name="w3_s", align_bytes=64)
         g_s = keep.tile([P, S], U8, name="g_s", align_bytes=64)
@@ -66,8 +65,7 @@ def tile_moe_cas_glu_silu_kernel(
         banks = [psum.tile([P, BANK], F32, name="bank%d" % b) for b in range(8)]
         result = [keep.tile([P, T], F32, name="result%d" % n) for n in range(N // P)]
 
-        nc.vector.memset(x_s[:, 0:VECTOR_CLEARS].bitcast(I32), 0)
-        nc.gpsimd.memset(x_s[:, VECTOR_CLEARS:T].bitcast(I32), 0)
+        nc.vector.memset(x_s[:].bitcast(I32), 0)
         nc.vector.memset(ws[:].bitcast(I32), 0)
         nc.vector.memset(w3s_raw[:].bitcast(I32), 0)
         warm = keep.tile([P, 2], F32, name="warm")
@@ -84,9 +82,10 @@ def tile_moe_cas_glu_silu_kernel(
         nc.sync.dma_start(out=x_w[:, XA:T], in_=x_dram[:, XA:T])
         load_words(nc.sync, w1_raw[:], w1_words)
         load_scales(nc.sync, ws, 0, 2 * N, w1_scales)
-        load_words(nc.sync, w3_raw[:], w3_words)
         load_scales(nc.gpsimd, w3s_raw, 0, 0, w3_scales, range(2, 4))
-        load_scales(nc.sync, w3s_raw, 0, 0, w3_scales, range(0, 2))
+        load_scales(nc.sync, w3s_raw, 0, 0, w3_scales, range(0, 1))
+        load_words(nc.sync, w3_raw[:], w3_words)
+        load_scales(nc.sync, w3s_raw, 0, 0, w3_scales, range(1, 2))
         load_scales(nc.sync, ws, 0, N, w2_scales)
         load_words(nc.sync, w2_w[:], w2_words)
 
@@ -190,14 +189,14 @@ def tile_moe_cas_glu_silu_kernel(
         g0 = keep.tile([P, CHUNK], U32, name="g0", align_bytes=64)
         gather_words(g0[:], 0)
         permute_scales(nc.vector, w1_s, ws[:, 2 * N : 2 * N + H])
-        g1 = keep.tile([P, CHUNK], U32, name="g1", align_bytes=64)
-        gather_words(g1[:], 1)
+        g3 = keep.tile([P, CHUNK], U32, name="g3", align_bytes=64)
+        gather_words(g3[:], 3)
         permute_words(nc.vector, w3_w, w3_raw[:])
         permute_scales(nc.vector, w3_s, w3s_raw[:])
-        g23 = keep.tile([P, 2 * CHUNK], U32, name="stage", align_bytes=64)
-        gather_words(g23[:, 0:CHUNK], 2)
-        gather_words(g23[:, CHUNK : 2 * CHUNK], 3)
-        g_w = [g[:, j * TILE : (j + 1) * TILE] for g, k in ((g0, 2), (g1, 2), (g23, 4)) for j in range(k)]
+        g12 = keep.tile([P, 2 * CHUNK], U32, name="stage", align_bytes=64)
+        gather_words(g12[:, 0:CHUNK], 1)
+        gather_words(g12[:, CHUNK : 2 * CHUNK], 2)
+        g_w = [g[:, j * TILE : (j + 1) * TILE] for g, k in ((g0, 2), (g12, 4), (g3, 2)) for j in range(k)]
 
         early = keep.tile([P, 6 * BANK], F32, name="early", align_bytes=64)
         late = keep.tile([P, 15 * TILE], F32, name="late", align_bytes=64)
@@ -219,13 +218,13 @@ def tile_moe_cas_glu_silu_kernel(
             light_layer(0, piece * CHUNK, CHUNK, bank)
         light_layer(0, 2 * BANK, BANK, 1)
         light_layer(0, 3 * BANK, BANK, 3)
-        light_layer(1, 0, CHUNK, 0)
+        light_layer(1, 0, BANK, 0)
         s0 = gate(0, 4, tokens(early, 0))
         s1 = gate(1, 5, tokens(early, BANK))
-        s2 = gate(2, 7, tokens(early, 4 * BANK))
-        s3 = gate(3, 6, tokens(late, 11 * TILE // 2))
         product_on_vector(0, s0, h_even[:], 2)
         product_on_vector(1, s1, h_a, 1)
+        s2 = gate(2, 7, tokens(early, 4 * BANK))
+        s3 = gate(3, 6, tokens(late, 11 * TILE // 2))
         quantise(0, TILE, h_even[:])
         quantise(TILE, TILE, h_a)
         product_on_vector(2, s2, h_even[:], 3)
@@ -233,11 +232,10 @@ def tile_moe_cas_glu_silu_kernel(
         quantise(2 * TILE, TILE, h_even[:])
         quantise(3 * TILE, TILE, h_a)
         s4 = gate(4, 4, tokens(early, 2 * BANK))
-        u4 = value(4, 5, tokens(early, 3 * BANK))
-        product_on_gpsimd(s4, u4, h_a)
-        light_layer(1, CHUNK, CHUNK, 6)
         z00 = second_layer(0, 0, CHUNK, z_tile("z00"), 2)
         scatter(0, 0, CHUNK, z00)
+        u4 = value(4, 5, tokens(early, 3 * BANK))
+        product_on_gpsimd(s4, u4, h_a)
         s5 = gate(5, 7, tokens(late, 7 * TILE // 2))
         u5 = value(5, 3, tokens(late, 15 * TILE // 2))
         product_on_gpsimd(s5, u5, h_b)
@@ -246,14 +244,14 @@ def tile_moe_cas_glu_silu_kernel(
         quantise(4 * TILE, CHUNK, h_pair[:])
         light_layer(1, BANK, BANK, 5)
         light_layer(1, 2 * BANK, BANK, 0)
-        light_layer(1, 3 * BANK, BANK, 2)
+        light_layer(1, 3 * BANK, BANK, 7)
         z10 = second_layer(1, 0, 3 * TILE, late[:, 4 * TILE : 7 * TILE], 1)
         scatter(1, 0, 3 * TILE, z10)
-        s6 = gate(6, 7, tokens(late, 0))
+        s6 = gate(6, 6, tokens(late, 0))
         u6 = value(6, 3, tokens(late, 11 * TILE))
         product_on_gpsimd(s6, u6, h_a)
         s7 = gate(7, 4, tokens(late, 7 * TILE))
-        z02 = second_layer(0, 2 * CHUNK, CHUNK, z_tile("z02"), 6)
+        z02 = second_layer(0, 2 * CHUNK, CHUNK, z_tile("z02"), 2)
         scatter(0, 2 * CHUNK, CHUNK, z02)
         u7 = value(7, 1, tokens(early, 5 * BANK))
         product_on_gpsimd(s7, u7, h_b)
@@ -264,7 +262,7 @@ def tile_moe_cas_glu_silu_kernel(
         scatter(0, 3 * CHUNK, CHUNK, z03)
         nc.sync.dma_start(out=out[0:P, :], in_=result[0][:])
         z12 = keep.tile([P, 3 * TILE], F32, name="z12", align_bytes=64)
-        second_layer(1, 5 * TILE, 3 * TILE, z12[:], 2)
+        second_layer(1, 5 * TILE, 3 * TILE, z12[:], 7)
         scatter(1, 5 * TILE, 3 * TILE, z12[:])
         nc.sync.dma_start(out=out[P : 2 * P, 0 : T // 2], in_=result[1][:, 0 : T // 2])
         nc.scalar.dma_start(out=out[P : 2 * P, T // 2 : T], in_=result[1][:, T // 2 : T])

@@ -52,11 +52,11 @@ def tile_moe_cas_glu_silu_kernel(
         w_w = keep.tile([P, N], I32, name="w_w", align_bytes=64)
         w2_w = keep.tile([P, N], I32, name="w2_w", align_bytes=64)
         w1_raw = keep.tile([P, H], I32, name="w1_raw", align_bytes=64)
-        w3_raw = keep.tile([P, H], I32, name="stage", align_bytes=64)
+        w3_raw = keep.tile([P, H], I32, name="w3_raw", align_bytes=64)
         w1_w = keep.tile([P, H], I32, name="w1_w", align_bytes=64)
         w3_w = keep.tile([P, H], I32, name="w3_w", align_bytes=64)
         ws = keep.tile([P, 2 * N + H], U8, name="ws", align_bytes=64)
-        w3s_raw = keep.tile([P, H], U8, name="w3s_raw", align_bytes=64)
+        w3s_raw = keep.tile([P, H], U8, name="stage", align_bytes=64)
         w1_s = keep.tile([P, H], U8, name="w1_s", align_bytes=64)
         w3_s = keep.tile([P, H], U8, name="w3_s", align_bytes=64)
         g_s = keep.tile([P, S], U8, name="g_s", align_bytes=64)
@@ -83,9 +83,8 @@ def tile_moe_cas_glu_silu_kernel(
         load_words(nc.sync, w1_raw[:], w1_words)
         load_scales(nc.sync, ws, 0, 2 * N, w1_scales)
         load_scales(nc.gpsimd, w3s_raw, 0, 0, w3_scales, range(2, 4))
-        load_scales(nc.sync, w3s_raw, 0, 0, w3_scales, range(0, 1))
         load_words(nc.sync, w3_raw[:], w3_words)
-        load_scales(nc.sync, w3s_raw, 0, 0, w3_scales, range(1, 2))
+        load_scales(nc.sync, w3s_raw, 0, 0, w3_scales, range(0, 2))
         load_scales(nc.sync, ws, 0, N, w2_scales)
         load_words(nc.sync, w2_w[:], w2_words)
 

@@ -203,16 +203,6 @@ def tile_moe_cas_glu_silu_kernel(
         h_pair = keep.tile([P, CHUNK, PACK], BF16, name="h_pair", align_bytes=64)
         h_a = h_pair[:, 0:TILE, :]
         h_b = h_pair[:, TILE:CHUNK, :]
-        for r in range(5):
-            nc.tensor.matmul_mx(
-                out=banks[5][:, 0:CHUNK],
-                lhsT=w_w[:, 0:P].bitcast(FP8X4),
-                lhsT_scale=x_s[:, 0:P],
-                rhs=w_w[:].bitcast(FP8X4),
-                rhs_scale=x_s[:, 0:CHUNK],
-                start=True,
-                stop=True,
-            )
         for piece, bank in enumerate((0, 7, 6, 2)):
             light_layer(0, piece * CHUNK, CHUNK, bank)
         light_layer(0, 2 * BANK, BANK, 1)

@@ -21,7 +21,7 @@ BANK = 512
 TILE = 128
 CHUNK = 256
 PER_COLUMN = 16
-XA = 1280
+XA = 1408
 
 
 def load_words(queue, tile, words):
@@ -81,10 +81,11 @@ def tile_moe_cas_glu_silu_kernel(
         load_scales(nc.sync, ws, 0, 0, w_scales, range(1, 4))
         nc.sync.dma_start(out=x_w[:, XA:T], in_=x_dram[:, XA:T])
         load_words(nc.sync, w1_raw[:], w1_words)
-        load_scales(nc.sync, ws, 0, 2 * N, w1_scales)
-        load_scales(nc.gpsimd, w3s_raw, 0, 0, w3_scales, range(2, 4))
+        load_scales(nc.sync, ws, 0, 2 * N, w1_scales, range(0, 3))
+        load_scales(nc.gpsimd, ws, 0, 2 * N, w1_scales, range(3, 4))
         load_words(nc.sync, w3_raw[:], w3_words)
-        load_scales(nc.sync, w3s_raw, 0, 0, w3_scales, range(0, 2))
+        load_scales(nc.gpsimd, w3s_raw, 0, 0, w3_scales, range(3, 4))
+        load_scales(nc.sync, w3s_raw, 0, 0, w3_scales, range(0, 3))
         load_scales(nc.sync, ws, 0, N, w2_scales)
         load_words(nc.sync, w2_w[:], w2_words)
 

@@ -13,6 +13,7 @@ U16 = mybir.dt.uint16
 U8 = mybir.dt.uint8
 FP8X4 = mybir.dt.float8_e4m3fn_x4
 SILU = mybir.ActivationFunctionType.Silu
+COPY = mybir.ActivationFunctionType.Copy
 MULT = mybir.AluOpType.mult
 
 P = 128
@@ -20,6 +21,8 @@ PACK = 4
 BANK = 512
 TILE = 128
 CHUNK = 256
+HALF = 512
+LONG = 384
 PER_COLUMN = 16
 XA = 1408
 
@@ -28,12 +31,11 @@ def load_words(queue, tile, words):
     queue.dma_start(out=tile, in_=words[0].rearrange("p n d -> p (n d)").bitcast(I32))
 
 
-def load_scales(queue, tile, first_row, first_col, scales, quadrants=range(4)):
+def load_scales(queue, tile, first_col, scales, quadrants=range(4)):
     width = scales.shape[2]
     for q in quadrants:
-        rows = slice(32 * q + first_row, 32 * q + first_row + 4)
         queue.dma_start(
-            out=tile[rows, first_col : first_col + width].bitcast(I32),
+            out=tile[32 * q : 32 * q + 4, first_col : first_col + width].bitcast(I32),
             in_=scales[0, 4 * q : 4 * q + 4, :].bitcast(I32),
         )
 
@@ -54,16 +56,18 @@ def tile_moe_cas_glu_silu_kernel(
         w1_raw = keep.tile([P, H], I32, name="w1_raw", align_bytes=64)
         w3_raw = keep.tile([P, H], I32, name="w3_raw", align_bytes=64)
         w1_w = keep.tile([P, H], I32, name="w1_w", align_bytes=64)
-        w3_w = keep.tile([P, H], I32, name="w3_w", align_bytes=64)
+        w3_w = keep.tile([P, H], I32, name="w3_then_h", align_bytes=64)
         ws = keep.tile([P, 2 * N + H], U8, name="ws", align_bytes=64)
         w3s_raw = keep.tile([P, H], U8, name="stage", align_bytes=64)
         w1_s = keep.tile([P, H], U8, name="w1_s", align_bytes=64)
         w3_s = keep.tile([P, H], U8, name="w3_s", align_bytes=64)
         g_s = keep.tile([P, S], U8, name="g_s", align_bytes=64)
-        h_w = keep.tile([P, S], U32, name="h_w", align_bytes=64)
         h_s = keep.tile([P, S], U8, name="h_s", align_bytes=64)
+        h = keep.tile([P, S * PACK], BF16, name="h", align_bytes=64)
+        gates = [keep.tile([P, BANK], F32, name="gate%d" % j, align_bytes=64) for j in range(S // TILE)]
         banks = [psum.tile([P, BANK], F32, name="bank%d" % b) for b in range(8)]
         result = [keep.tile([P, T], F32, name="result%d" % n) for n in range(N // P)]
+        z_high = keep.tile([P, S], F32, name="z_high", align_bytes=64)
 
         nc.vector.memset(x_s[:].bitcast(I32), 0)
         nc.vector.memset(ws[:].bitcast(I32), 0)
@@ -75,25 +79,25 @@ def tile_moe_cas_glu_silu_kernel(
         nc.scalar.activation(warm[:, 1:2], warm[:, 0:1], SILU)
         nc.sync.dma_start(offsets[:], offs)
         load_words(nc.sync, w_w[:], w_words)
-        load_scales(nc.sync, x_s, 0, 0, x_scales)
-        load_scales(nc.sync, ws, 0, 0, w_scales, range(0, 1))
+        load_scales(nc.sync, x_s, 0, x_scales)
+        load_scales(nc.sync, ws, 0, w_scales, range(0, 1))
         nc.sync.dma_start(out=x_w[:, 0:XA], in_=x_dram[:, 0:XA])
-        load_scales(nc.sync, ws, 0, 0, w_scales, range(1, 4))
+        load_scales(nc.sync, ws, 0, w_scales, range(1, 4))
         nc.sync.dma_start(out=x_w[:, XA:T], in_=x_dram[:, XA:T])
         load_words(nc.sync, w1_raw[:], w1_words)
-        load_scales(nc.sync, ws, 0, 2 * N, w1_scales, range(0, 3))
-        load_scales(nc.gpsimd, ws, 0, 2 * N, w1_scales, range(3, 4))
+        load_scales(nc.sync, ws, 2 * N, w1_scales, range(0, 3))
+        load_scales(nc.gpsimd, ws, 2 * N, w1_scales, range(3, 4))
         load_words(nc.sync, w3_raw[:], w3_words)
-        load_scales(nc.gpsimd, w3s_raw, 0, 0, w3_scales, range(3, 4))
-        load_scales(nc.sync, w3s_raw, 0, 0, w3_scales, range(0, 3))
-        load_scales(nc.sync, ws, 0, N, w2_scales)
+        load_scales(nc.gpsimd, w3s_raw, 0, w3_scales, range(3, 4))
+        load_scales(nc.sync, w3s_raw, 0, w3_scales, range(0, 3))
+        load_scales(nc.sync, ws, N, w2_scales)
         load_words(nc.sync, w2_w[:], w2_words)
 
         def offset_columns(first, count):
             return offsets[:, first // PER_COLUMN : (first + count) // PER_COLUMN]
 
-        def gather_words(out_words, c):
-            nc.vector.tensor_copy(out_words, x_w[:].bitcast(U32).indirect(offset_columns(c * CHUNK, CHUNK)))
+        def gather_words(words, first):
+            nc.vector.tensor_copy(words, x_w[:].bitcast(U32).indirect(offset_columns(first, CHUNK)))
 
         def permute_words(engine, words, raw):
             engine.tensor_copy(
@@ -121,9 +125,10 @@ def tile_moe_cas_glu_silu_kernel(
             nc.scalar.copy(result[n][:, cols], y)
 
         def first_layer_sums(bank, words, plane, tile):
+            sums = banks[bank][:].rearrange("p (t j) -> p t j", t=PACK)
             for t in range(PACK):
                 nc.tensor.matmul_mx(
-                    out=bank[:, t, :],
+                    out=sums[:, t, :],
                     lhsT=words[:, t * P : (t + 1) * P].bitcast(FP8X4),
                     lhsT_scale=plane[:, t * P : (t + 1) * P],
                     rhs=g_w[tile].bitcast(FP8X4),
@@ -131,128 +136,102 @@ def tile_moe_cas_glu_silu_kernel(
                     start=True,
                     stop=True,
                 )
+            return sums.rearrange("p t j -> p j t")
 
-        def gate(tile, bank, s):
-            a = banks[bank][:].rearrange("p (t j) -> p t j", t=PACK)
-            first_layer_sums(a, w1_w, w1_s, tile)
-            nc.scalar.activation(s, a.rearrange("p t j -> p j t"), SILU)
-            return s
+        def by_token(columns):
+            return columns.rearrange("p (j t) -> p j t", t=PACK)
 
-        def product_on_vector(tile, s, h, bank):
-            b = banks[bank][:].rearrange("p (t j) -> p t j", t=PACK)
-            first_layer_sums(b, w3_w, w3_s, tile)
-            nc.vector.tensor_tensor(h, b.rearrange("p t j -> p j t"), s, MULT)
+        def gate(tile, bank):
+            a = first_layer_sums(bank, w1_w, w1_s, tile)
+            nc.scalar.activation(by_token(gates[tile][:]), a, SILU)
 
-        def value(tile, bank, u):
-            b = banks[bank][:].rearrange("p (t j) -> p t j", t=PACK)
-            first_layer_sums(b, w3_w, w3_s, tile)
-            nc.scalar.copy(u, b.rearrange("p t j -> p j t"))
-            return u
+        def value(tile, bank):
+            return first_layer_sums(bank, w3_w, w3_s, tile)
 
-        def product_on_gpsimd(s, u, h):
-            nc.gpsimd.tensor_tensor(h, u, s, MULT)
+        def product(tile, b):
+            nc.vector.tensor_tensor(by_token(h[:, tile * BANK : (tile + 1) * BANK]), b, by_token(gates[tile][:]), MULT)
 
-        def quantise(first, count, h):
-            cols = slice(first, first + count)
+        def quantise(half, name):
+            cols = slice(half * HALF, (half + 1) * HALF)
+            words = keep.tile([P, HALF], U32, name=name, align_bytes=64)
             nc.vector.quantize_mx(
-                out=h_w[:, cols].bitcast(FP8X4), scales=h_s[:, cols], in_=h.rearrange("p j t -> p (j t)")
+                out=words[:].bitcast(FP8X4), scales=h_s[:, cols], in_=h[:, half * HALF * PACK : (half + 1) * HALF * PACK]
             )
+            return words
 
-        def second_layer(n, first, count, z, bank):
-            for done in range(0, count, CHUNK):
-                width = min(CHUNK, count - done)
-                cols = slice(first + done, first + done + width)
-                nc.tensor.matmul_mx(
-                    out=banks[bank][:, done : done + width],
-                    lhsT=w2_w[:, n * P : (n + 1) * P].bitcast(FP8X4),
-                    lhsT_scale=ws[:, N + n * P : N + (n + 1) * P],
-                    rhs=h_w[:, cols].bitcast(FP8X4),
-                    rhs_scale=h_s[:, cols],
-                    start=True,
-                    stop=True,
-                )
-            nc.scalar.copy(z, banks[bank][:, 0:count])
-            return z
+        def second_layer(n, half, words, bank, z):
+            cols = slice(half * HALF, (half + 1) * HALF)
+            nc.tensor.matmul_mx(
+                out=banks[bank][:],
+                lhsT=w2_w[:, n * P : (n + 1) * P].bitcast(FP8X4),
+                lhsT_scale=ws[:, N + n * P : N + (n + 1) * P],
+                rhs=words[:].bitcast(FP8X4),
+                rhs_scale=h_s[:, cols],
+                start=True,
+                stop=True,
+            )
+            nc.scalar.copy(z, banks[bank][:])
 
-        def scatter(n, first, count, z):
-            nc.vector.tensor_copy(result[n][:].indirect(offset_columns(first, count)), z)
+        def scatter_on_vector(half, z):
+            nc.vector.tensor_copy(result[0][:].indirect(offset_columns(half * HALF, HALF)), z)
 
-        def z_tile(name):
-            z = keep.tile([P, CHUNK], F32, name=name, align_bytes=64)
-            return z[:]
-
-        def tokens(tile, first):
-            return tile[:, first : first + BANK].rearrange("p (j t) -> p j t", t=PACK)
+        def scatter_on_scalar(first, count):
+            nc.scalar.activation(
+                result[1][:].indirect(offset_columns(first, count)), z_high[:, first : first + count], COPY
+            )
 
         nc.vector.tensor_copy(g_s[:], x_s[:].indirect(offsets[:]))
         permute_words(nc.vector, w1_w, w1_raw[:])
-        g0 = keep.tile([P, CHUNK], U32, name="g0", align_bytes=64)
-        gather_words(g0[:], 0)
+        g_first = keep.tile([P, CHUNK], U32, name="g_first", align_bytes=64)
+        gather_words(g_first[:], 0)
         permute_scales(nc.vector, w1_s, ws[:, 2 * N : 2 * N + H])
-        g3 = keep.tile([P, CHUNK], U32, name="g3", align_bytes=64)
-        gather_words(g3[:], 3)
+        g_last = keep.tile([P, CHUNK], U32, name="g_last", align_bytes=64)
+        gather_words(g_last[:], 3 * CHUNK)
         permute_words(nc.vector, w3_w, w3_raw[:])
         permute_scales(nc.vector, w3_s, w3s_raw[:])
-        g12 = keep.tile([P, 2 * CHUNK], U32, name="stage", align_bytes=64)
-        gather_words(g12[:, 0:CHUNK], 1)
-        gather_words(g12[:, CHUNK : 2 * CHUNK], 2)
-        g_w = [g[:, j * TILE : (j + 1) * TILE] for g, k in ((g0, 2), (g12, 4), (g3, 2)) for j in range(k)]
+        g_mid = keep.tile([P, 2 * CHUNK], U32, name="stage", align_bytes=64)
+        gather_words(g_mid[:, 0:CHUNK], CHUNK)
+        gather_words(g_mid[:, CHUNK : 2 * CHUNK], 2 * CHUNK)
+        g_w = [g[:, j * TILE : (j + 1) * TILE] for g, k in ((g_first, 2), (g_mid, 4), (g_last, 2)) for j in range(k)]
 
-        early = keep.tile([P, 6 * BANK], F32, name="early", align_bytes=64)
-        late = keep.tile([P, 15 * TILE], F32, name="late", align_bytes=64)
-        h_even = keep.tile([P, TILE, PACK], BF16, name="h_even", align_bytes=64)
-        h_pair = keep.tile([P, CHUNK, PACK], BF16, name="h_pair", align_bytes=64)
-        h_a = h_pair[:, 0:TILE, :]
-        h_b = h_pair[:, TILE:CHUNK, :]
-        for piece, bank in enumerate((0, 7, 6, 2)):
-            light_layer(0, piece * CHUNK, CHUNK, bank)
-        light_layer(0, 2 * BANK, BANK, 1)
-        light_layer(0, 3 * BANK, BANK, 3)
-        light_layer(1, 0, BANK, 0)
-        s0 = gate(0, 4, tokens(early, 0))
-        s1 = gate(1, 5, tokens(early, BANK))
-        product_on_vector(0, s0, h_even[:], 2)
-        product_on_vector(1, s1, h_a, 1)
-        s2 = gate(2, 7, tokens(early, 4 * BANK))
-        s3 = gate(3, 6, tokens(late, 11 * TILE // 2))
-        quantise(0, TILE, h_even[:])
-        quantise(TILE, TILE, h_a)
-        product_on_vector(2, s2, h_even[:], 3)
-        product_on_vector(3, s3, h_a, 0)
-        quantise(2 * TILE, TILE, h_even[:])
-        quantise(3 * TILE, TILE, h_a)
-        s4 = gate(4, 4, tokens(early, 2 * BANK))
-        z00 = second_layer(0, 0, CHUNK, z_tile("z00"), 2)
-        scatter(0, 0, CHUNK, z00)
-        u4 = value(4, 5, tokens(early, 3 * BANK))
-        product_on_gpsimd(s4, u4, h_a)
-        s5 = gate(5, 7, tokens(late, 7 * TILE // 2))
-        u5 = value(5, 3, tokens(late, 15 * TILE // 2))
-        product_on_gpsimd(s5, u5, h_b)
-        z01 = second_layer(0, CHUNK, CHUNK, z_tile("z01"), 4)
-        scatter(0, CHUNK, CHUNK, z01)
-        quantise(4 * TILE, CHUNK, h_pair[:])
-        light_layer(1, BANK, BANK, 5)
-        light_layer(1, 2 * BANK, BANK, 0)
-        light_layer(1, 3 * BANK, BANK, 7)
-        z10 = second_layer(1, 0, 3 * TILE, late[:, 4 * TILE : 7 * TILE], 1)
-        scatter(1, 0, 3 * TILE, z10)
-        s6 = gate(6, 6, tokens(late, 0))
-        u6 = value(6, 3, tokens(late, 11 * TILE))
-        product_on_gpsimd(s6, u6, h_a)
-        s7 = gate(7, 4, tokens(late, 7 * TILE))
-        z02 = second_layer(0, 2 * CHUNK, CHUNK, z_tile("z02"), 2)
-        scatter(0, 2 * CHUNK, CHUNK, z02)
-        u7 = value(7, 1, tokens(early, 5 * BANK))
-        product_on_gpsimd(s7, u7, h_b)
-        quantise(6 * TILE, CHUNK, h_pair[:])
-        z11 = second_layer(1, 3 * TILE, CHUNK, early[:, 5 * BANK : 5 * BANK + CHUNK], 5)
-        scatter(1, 3 * TILE, CHUNK, z11)
-        z03 = second_layer(0, 3 * CHUNK, CHUNK, z_tile("z03"), 0)
-        scatter(0, 3 * CHUNK, CHUNK, z03)
+        for piece in range(4):
+            light_layer(0, piece * CHUNK, CHUNK, piece)
+        light_layer(0, 2 * BANK, BANK, 4)
+        light_layer(0, 3 * BANK, BANK, 5)
+        light_layer(1, 0, BANK, 6)
+        gate(0, 7)
+        gate(1, 0)
+        product(0, value(0, 1))
+        product(1, value(1, 2))
+        gate(2, 3)
+        gate(3, 4)
+        product(2, value(2, 5))
+        gate(4, 6)
+        product(3, value(3, 7))
+        light_layer(1, BANK, BANK, 3)
+        gate(5, 0)
+        late_values = [value(4, 1), value(5, 2), value(6, 5), value(7, 7)]
+        product(4, late_values[0])
+        first_half = quantise(0, "w3_then_h")
+        light_layer(1, 2 * BANK, BANK, 6)
+        gate(6, 4)
+        gate(7, 0)
+        product(5, late_values[1])
+        product(6, late_values[2])
+        product(7, late_values[3])
+        light_layer(1, 3 * BANK, BANK, 3)
+        second_layer(1, 0, first_half, 6, z_high[:, 0:HALF])
+        second_half = quantise(1, "h_second")
+        z_first = keep.tile([P, HALF], F32, name="gate7", align_bytes=64)
+        second_layer(0, 0, first_half, 4, z_first[:])
+        scatter_on_vector(0, z_first[:])
+        z_second = keep.tile([P, HALF], F32, name="z_second", align_bytes=64)
+        second_layer(0, 1, second_half, 1, z_second[:])
+        second_layer(1, 1, second_half, 2, z_high[:, HALF:S])
+        scatter_on_vector(1, z_second[:])
         nc.sync.dma_start(out=out[0:P, :], in_=result[0][:])
-        z12 = keep.tile([P, 3 * TILE], F32, name="z12", align_bytes=64)
-        second_layer(1, 5 * TILE, 3 * TILE, z12[:], 7)
-        scatter(1, 5 * TILE, 3 * TILE, z12[:])
+        scatter_on_scalar(0, LONG)
+        scatter_on_scalar(LONG, LONG)
+        scatter_on_scalar(2 * LONG, CHUNK)
         nc.sync.dma_start(out=out[P : 2 * P, 0 : T // 2], in_=result[1][:, 0 : T // 2])
         nc.scalar.dma_start(out=out[P : 2 * P, T // 2 : T], in_=result[1][:, T // 2 : T])

@@ -56,7 +56,7 @@ def tile_moe_cas_glu_silu_kernel(
         w1_raw = keep.tile([P, H], I32, name="w1_raw", align_bytes=64)
         w3_raw = keep.tile([P, H], I32, name="w3_raw", align_bytes=64)
         w1_w = keep.tile([P, H], I32, name="w1_w", align_bytes=64)
-        w3_w = keep.tile([P, H], I32, name="w3_then_h", align_bytes=64)
+        w3_w = keep.tile([P, H], I32, name="w3_w", align_bytes=64)
         ws = keep.tile([P, 2 * N + H], U8, name="ws", align_bytes=64)
         w3s_raw = keep.tile([P, H], U8, name="stage", align_bytes=64)
         w1_s = keep.tile([P, H], U8, name="w1_s", align_bytes=64)
@@ -122,7 +122,7 @@ def tile_moe_cas_glu_silu_kernel(
                 start=True,
                 stop=True,
             )
-            nc.scalar.copy(result[n][:, cols], y)
+            return result[n][:, cols], y
 
         def first_layer_sums(bank, words, plane, tile):
             sums = banks[bank][:].rearrange("p (t j) -> p t j", t=PACK)
@@ -141,8 +141,10 @@ def tile_moe_cas_glu_silu_kernel(
         def by_token(columns):
             return columns.rearrange("p (j t) -> p j t", t=PACK)
 
-        def gate(tile, bank):
-            a = first_layer_sums(bank, w1_w, w1_s, tile)
+        def gate_sums(tile, bank):
+            return first_layer_sums(bank, w1_w, w1_s, tile)
+
+        def silu(tile, a):
             nc.scalar.activation(by_token(gates[tile][:]), a, SILU)
 
         def value(tile, bank):
@@ -159,7 +161,7 @@ def tile_moe_cas_glu_silu_kernel(
             )
             return words
 
-        def second_layer(n, half, words, bank, z):
+        def second_layer(n, half, words, bank):
             cols = slice(half * HALF, (half + 1) * HALF)
             nc.tensor.matmul_mx(
                 out=banks[bank][:],
@@ -170,10 +172,10 @@ def tile_moe_cas_glu_silu_kernel(
                 start=True,
                 stop=True,
             )
-            nc.scalar.copy(z, banks[bank][:])
+            return banks[bank]
 
-        def scatter_on_vector(half, z):
-            nc.vector.tensor_copy(result[0][:].indirect(offset_columns(half * HALF, HALF)), z)
+        def scatter_on_vector(first, count, z):
+            nc.vector.tensor_copy(result[0][:].indirect(offset_columns(first, count)), z)
 
         def scatter_on_scalar(first, count):
             nc.scalar.activation(
@@ -195,43 +197,52 @@ def tile_moe_cas_glu_silu_kernel(
         g_w = [g[:, j * TILE : (j + 1) * TILE] for g, k in ((g_first, 2), (g_mid, 4), (g_last, 2)) for j in range(k)]
 
         for piece in range(4):
-            light_layer(0, piece * CHUNK, CHUNK, piece)
-        light_layer(0, 2 * BANK, BANK, 4)
-        light_layer(0, 3 * BANK, BANK, 5)
-        light_layer(1, 0, BANK, 6)
-        gate(0, 7)
-        gate(1, 0)
+            nc.scalar.copy(*light_layer(0, piece * CHUNK, CHUNK, piece))
+        nc.scalar.copy(*light_layer(0, 2 * BANK, BANK, 4))
+        nc.scalar.copy(*light_layer(0, 3 * BANK, BANK, 5))
+        nc.scalar.copy(*light_layer(1, 0, BANK, 6))
+        silu(0, gate_sums(0, 7))
+        silu(1, gate_sums(1, 0))
         product(0, value(0, 1))
         product(1, value(1, 2))
-        gate(2, 3)
-        gate(3, 4)
+        silu(2, gate_sums(2, 3))
+        silu(3, gate_sums(3, 4))
         product(2, value(2, 5))
-        gate(4, 6)
+        silu(4, gate_sums(4, 6))
         product(3, value(3, 7))
-        light_layer(1, BANK, BANK, 3)
-        gate(5, 0)
-        late_values = [value(4, 1), value(5, 2), value(6, 5), value(7, 7)]
-        product(4, late_values[0])
-        first_half = quantise(0, "w3_then_h")
-        light_layer(1, 2 * BANK, BANK, 6)
-        gate(6, 4)
-        gate(7, 0)
-        product(5, late_values[1])
-        product(6, late_values[2])
-        product(7, late_values[3])
-        light_layer(1, 3 * BANK, BANK, 3)
-        second_layer(1, 0, first_half, 6, z_high[:, 0:HALF])
+        a5 = gate_sums(5, 0)
+        b4 = value(4, 1)
+        nc.scalar.copy(*light_layer(1, BANK, BANK, 3))
+        silu(5, a5)
+        b5 = value(5, 2)
+        a6 = gate_sums(6, 4)
+        b6 = value(6, 5)
+        nc.scalar.copy(*light_layer(1, 2 * BANK, BANK, 6))
+        silu(6, a6)
+        b7 = value(7, 7)
+        silu(7, gate_sums(7, 0))
+        product(4, b4)
+        first_half = quantise(0, "h_first")
+        product(5, b5)
+        product(6, b6)
+        product(7, b7)
+        sums = second_layer(0, 0, first_half, 4)
+        z_a = keep.tile([P, CHUNK], F32, name="z_a", align_bytes=64)
+        nc.scalar.copy(z_a[:], sums[:, 0:CHUNK])
+        scatter_on_vector(0, CHUNK, z_a[:])
+        nc.scalar.copy(*light_layer(1, 3 * BANK, BANK, 3))
+        nc.scalar.copy(z_high[:, 0:HALF], second_layer(1, 0, first_half, 1)[:])
         second_half = quantise(1, "h_second")
-        z_first = keep.tile([P, HALF], F32, name="gate7", align_bytes=64)
-        second_layer(0, 0, first_half, 4, z_first[:])
-        scatter_on_vector(0, z_first[:])
-        z_second = keep.tile([P, HALF], F32, name="z_second", align_bytes=64)
-        second_layer(0, 1, second_half, 1, z_second[:])
-        second_layer(1, 1, second_half, 2, z_high[:, HALF:S])
-        scatter_on_vector(1, z_second[:])
+        z_b = keep.tile([P, CHUNK], F32, name="gate7", align_bytes=64)
+        nc.scalar.copy(z_b[:], sums[:, CHUNK:HALF])
+        scatter_on_vector(CHUNK, CHUNK, z_b[:])
+        scatter_on_scalar(0, CHUNK)
+        z_c = keep.tile([P, HALF], F32, name="z_c", align_bytes=64)
+        nc.scalar.copy(z_c[:], second_layer(0, 1, second_half, 6)[:])
+        nc.scalar.copy(z_high[:, HALF:S], second_layer(1, 1, second_half, 2)[:])
+        scatter_on_vector(HALF, HALF, z_c[:])
         nc.sync.dma_start(out=out[0:P, :], in_=result[0][:])
-        scatter_on_scalar(0, LONG)
-        scatter_on_scalar(LONG, LONG)
-        scatter_on_scalar(2 * LONG, CHUNK)
+        scatter_on_scalar(CHUNK, LONG)
+        scatter_on_scalar(CHUNK + LONG, LONG)
         nc.sync.dma_start(out=out[P : 2 * P, 0 : T // 2], in_=result[1][:, 0 : T // 2])
         nc.scalar.dma_start(out=out[P : 2 * P, T // 2 : T], in_=result[1][:, T // 2 : T])

@@ -96,13 +96,14 @@ def tile_moe_cas_glu_silu_kernel(
         def offset_columns(first, count):
             return offsets[:, first // PER_COLUMN : (first + count) // PER_COLUMN]
 
-        def gather_words(words, first):
-            nc.vector.tensor_copy(words, x_w[:].bitcast(U32).indirect(offset_columns(first, CHUNK)))
+        def gather_words(name, first, count):
+            words = keep.tile([P, count], U32, name=name, align_bytes=64)
+            nc.vector.tensor_copy(words[:], x_w[:].bitcast(U32).indirect(offset_columns(first, count)))
+            return [words[:, j : j + TILE] for j in range(0, count, TILE)]
 
         def permute_words(engine, words, raw):
             engine.tensor_copy(
-                words[:].rearrange("p (t c i) -> p c t i", t=PACK, i=PACK),
-                raw.rearrange("p (c i t) -> p c t i", t=PACK, i=PACK),
+                words[:].rearrange("p (t m) -> p t m", t=PACK), raw.rearrange("p (m t) -> p t m", t=PACK)
             )
 
         def permute_scales(engine, plane, raw):
@@ -183,65 +184,63 @@ def tile_moe_cas_glu_silu_kernel(
             )
 
         nc.vector.tensor_copy(g_s[:], x_s[:].indirect(offsets[:]))
-        permute_words(nc.vector, w1_w, w1_raw[:])
-        g_first = keep.tile([P, CHUNK], U32, name="g_first", align_bytes=64)
-        gather_words(g_first[:], 0)
-        permute_scales(nc.vector, w1_s, ws[:, 2 * N : 2 * N + H])
-        g_last = keep.tile([P, CHUNK], U32, name="g_last", align_bytes=64)
-        gather_words(g_last[:], 3 * CHUNK)
-        permute_words(nc.vector, w3_w, w3_raw[:])
+        permute_words(nc.gpsimd, w1_w, w1_raw[:])
+        permute_scales(nc.gpsimd, w1_s, ws[:, 2 * N : 2 * N + H])
+        permute_words(nc.gpsimd, w3_w, w3_raw[:])
+        g_early = gather_words("g_early", 0, 3 * TILE)
+        g_late = gather_words("g_late", HALF, HALF)
         permute_scales(nc.vector, w3_s, w3s_raw[:])
-        g_mid = keep.tile([P, 2 * CHUNK], U32, name="stage", align_bytes=64)
-        gather_words(g_mid[:, 0:CHUNK], CHUNK)
-        gather_words(g_mid[:, CHUNK : 2 * CHUNK], 2 * CHUNK)
-        g_w = [g[:, j * TILE : (j + 1) * TILE] for g, k in ((g_first, 2), (g_mid, 4), (g_last, 2)) for j in range(k)]
+        g_w = g_early + gather_words("stage", 3 * TILE, TILE) + g_late
 
         for piece in range(4):
             nc.scalar.copy(*light_layer(0, piece * CHUNK, CHUNK, piece))
         nc.scalar.copy(*light_layer(0, 2 * BANK, BANK, 4))
         nc.scalar.copy(*light_layer(0, 3 * BANK, BANK, 5))
-        nc.scalar.copy(*light_layer(1, 0, BANK, 6))
-        silu(0, gate_sums(0, 7))
-        silu(1, gate_sums(1, 0))
+        silu(0, gate_sums(0, 6))
+        silu(1, gate_sums(1, 7))
+        silu(2, gate_sums(2, 0))
         product(0, value(0, 1))
         product(1, value(1, 2))
-        silu(2, gate_sums(2, 3))
-        silu(3, gate_sums(3, 4))
-        product(2, value(2, 5))
-        silu(4, gate_sums(4, 6))
-        product(3, value(3, 7))
-        a5 = gate_sums(5, 0)
-        b4 = value(4, 1)
-        nc.scalar.copy(*light_layer(1, BANK, BANK, 3))
-        silu(5, a5)
-        b5 = value(5, 2)
-        a6 = gate_sums(6, 4)
-        b6 = value(6, 5)
-        nc.scalar.copy(*light_layer(1, 2 * BANK, BANK, 6))
-        silu(6, a6)
-        b7 = value(7, 7)
-        silu(7, gate_sums(7, 0))
+        silu(3, gate_sums(3, 3))
+        product(2, value(2, 4))
+        silu(4, gate_sums(4, 1))
+        product(3, value(3, 5))
+        nc.scalar.copy(*light_layer(1, 0, BANK, 2))
+        b4 = value(4, 6)
+        silu(5, gate_sums(5, 3))
         product(4, b4)
         first_half = quantise(0, "h_first")
+        silu(6, gate_sums(6, 4))
+        b5 = value(5, 7)
+        silu(7, gate_sums(7, 1))
         product(5, b5)
-        product(6, b6)
-        product(7, b7)
-        sums = second_layer(0, 0, first_half, 4)
+        product(6, value(6, 5))
+        product(7, value(7, 6))
+        low = second_layer(0, 0, first_half, 0)
         z_a = keep.tile([P, CHUNK], F32, name="z_a", align_bytes=64)
-        nc.scalar.copy(z_a[:], sums[:, 0:CHUNK])
+        nc.scalar.copy(z_a[:], low[:, 0:CHUNK])
         scatter_on_vector(0, CHUNK, z_a[:])
-        nc.scalar.copy(*light_layer(1, 3 * BANK, BANK, 3))
-        nc.scalar.copy(z_high[:, 0:HALF], second_layer(1, 0, first_half, 1)[:])
         second_half = quantise(1, "h_second")
         z_b = keep.tile([P, CHUNK], F32, name="gate7", align_bytes=64)
-        nc.scalar.copy(z_b[:], sums[:, CHUNK:HALF])
+        nc.scalar.copy(z_b[:], low[:, CHUNK:HALF])
         scatter_on_vector(CHUNK, CHUNK, z_b[:])
+        nc.scalar.copy(*light_layer(1, BANK, BANK, 2))
+        nc.scalar.copy(*light_layer(1, 2 * BANK, BANK, 3))
+        high = second_layer(1, 0, first_half, 4)
+        nc.scalar.copy(z_high[:, 0:CHUNK], high[:, 0:CHUNK])
+        nc.scalar.copy(*light_layer(1, 3 * BANK, BANK, 1))
+        nc.scalar.copy(z_high[:, CHUNK:HALF], high[:, CHUNK:HALF])
         scatter_on_scalar(0, CHUNK)
+        low = second_layer(0, 1, second_half, 7)
+        high = second_layer(1, 1, second_half, 5)
         z_c = keep.tile([P, HALF], F32, name="z_c", align_bytes=64)
-        nc.scalar.copy(z_c[:], second_layer(0, 1, second_half, 6)[:])
-        nc.scalar.copy(z_high[:, HALF:S], second_layer(1, 1, second_half, 2)[:])
-        scatter_on_vector(HALF, HALF, z_c[:])
+        nc.vector.tensor_copy(z_c[:, 0:CHUNK], low[:, 0:CHUNK])
+        nc.vector.tensor_copy(z_c[:, CHUNK:HALF], low[:, CHUNK:HALF])
+        scatter_on_vector(HALF, CHUNK, z_c[:, 0:CHUNK])
+        scatter_on_vector(HALF + CHUNK, CHUNK, z_c[:, CHUNK:HALF])
         nc.sync.dma_start(out=out[0:P, :], in_=result[0][:])
+        nc.scalar.copy(z_high[:, HALF : HALF + CHUNK], high[:, 0:CHUNK])
+        nc.scalar.copy(z_high[:, HALF + CHUNK : S], high[:, CHUNK:HALF])
         scatter_on_scalar(CHUNK, LONG)
         scatter_on_scalar(CHUNK + LONG, LONG)
         nc.sync.dma_start(out=out[P : 2 * P, 0 : T // 2], in_=result[1][:, 0 : T // 2])

@@ -103,7 +103,8 @@ def tile_moe_cas_glu_silu_kernel(
 
         def permute_words(engine, words, raw):
             engine.tensor_copy(
-                words[:].rearrange("p (t m) -> p t m", t=PACK), raw.rearrange("p (m t) -> p t m", t=PACK)
+                words[:].rearrange("p (t c i) -> p c t i", t=PACK, i=PACK),
+                raw.rearrange("p (c i t) -> p c t i", t=PACK, i=PACK),
             )
 
         def permute_scales(engine, plane, raw):
@@ -184,38 +185,39 @@ def tile_moe_cas_glu_silu_kernel(
             )
 
         nc.vector.tensor_copy(g_s[:], x_s[:].indirect(offsets[:]))
-        permute_words(nc.gpsimd, w1_w, w1_raw[:])
-        permute_scales(nc.gpsimd, w1_s, ws[:, 2 * N : 2 * N + H])
-        permute_words(nc.gpsimd, w3_w, w3_raw[:])
-        g_early = gather_words("g_early", 0, 3 * TILE)
-        g_late = gather_words("g_late", HALF, HALF)
+        permute_words(nc.vector, w1_w, w1_raw[:])
+        g_first = gather_words("g_first", 0, CHUNK)
+        permute_scales(nc.vector, w1_s, ws[:, 2 * N : 2 * N + H])
+        g_last = gather_words("g_last", 3 * CHUNK, CHUNK)
+        permute_words(nc.vector, w3_w, w3_raw[:])
         permute_scales(nc.vector, w3_s, w3s_raw[:])
-        g_w = g_early + gather_words("stage", 3 * TILE, TILE) + g_late
+        g_w = g_first + gather_words("stage", CHUNK, HALF) + g_last
 
         for piece in range(4):
             nc.scalar.copy(*light_layer(0, piece * CHUNK, CHUNK, piece))
         nc.scalar.copy(*light_layer(0, 2 * BANK, BANK, 4))
         nc.scalar.copy(*light_layer(0, 3 * BANK, BANK, 5))
-        silu(0, gate_sums(0, 6))
-        silu(1, gate_sums(1, 7))
-        silu(2, gate_sums(2, 0))
+        nc.scalar.copy(*light_layer(1, 0, BANK, 6))
+        silu(0, gate_sums(0, 7))
+        silu(1, gate_sums(1, 0))
         product(0, value(0, 1))
         product(1, value(1, 2))
-        silu(3, gate_sums(3, 3))
-        product(2, value(2, 4))
-        silu(4, gate_sums(4, 1))
-        product(3, value(3, 5))
-        nc.scalar.copy(*light_layer(1, 0, BANK, 2))
-        b4 = value(4, 6)
-        silu(5, gate_sums(5, 3))
+        silu(2, gate_sums(2, 3))
+        silu(3, gate_sums(3, 4))
+        product(2, value(2, 5))
+        silu(4, gate_sums(4, 6))
+        product(3, value(3, 7))
+        silu(5, gate_sums(5, 0))
+        b4 = value(4, 1)
+        nc.scalar.copy(*light_layer(1, BANK, BANK, 3))
         product(4, b4)
         first_half = quantise(0, "h_first")
         silu(6, gate_sums(6, 4))
-        b5 = value(5, 7)
-        silu(7, gate_sums(7, 1))
+        b5 = value(5, 2)
+        silu(7, gate_sums(7, 6))
         product(5, b5)
         product(6, value(6, 5))
-        product(7, value(7, 6))
+        product(7, value(7, 7))
         low = second_layer(0, 0, first_half, 0)
         z_a = keep.tile([P, CHUNK], F32, name="z_a", align_bytes=64)
         nc.scalar.copy(z_a[:], low[:, 0:CHUNK])
@@ -224,15 +226,14 @@ def tile_moe_cas_glu_silu_kernel(
         z_b = keep.tile([P, CHUNK], F32, name="gate7", align_bytes=64)
         nc.scalar.copy(z_b[:], low[:, CHUNK:HALF])
         scatter_on_vector(CHUNK, CHUNK, z_b[:])
-        nc.scalar.copy(*light_layer(1, BANK, BANK, 2))
         nc.scalar.copy(*light_layer(1, 2 * BANK, BANK, 3))
         high = second_layer(1, 0, first_half, 4)
         nc.scalar.copy(z_high[:, 0:CHUNK], high[:, 0:CHUNK])
-        nc.scalar.copy(*light_layer(1, 3 * BANK, BANK, 1))
+        nc.scalar.copy(*light_layer(1, 3 * BANK, BANK, 6))
         nc.scalar.copy(z_high[:, CHUNK:HALF], high[:, CHUNK:HALF])
         scatter_on_scalar(0, CHUNK)
-        low = second_layer(0, 1, second_half, 7)
-        high = second_layer(1, 1, second_half, 5)
+        low = second_layer(0, 1, second_half, 1)
+        high = second_layer(1, 1, second_half, 2)
         z_c = keep.tile([P, HALF], F32, name="z_c", align_bytes=64)
         nc.vector.tensor_copy(z_c[:, 0:CHUNK], low[:, 0:CHUNK])
         nc.vector.tensor_copy(z_c[:, CHUNK:HALF], low[:, CHUNK:HALF])

@@ -98,7 +98,9 @@ def tile_moe_cas_glu_silu_kernel(
 
         def gather_words(name, first, count):
             words = keep.tile([P, count], U32, name=name, align_bytes=64)
-            nc.vector.tensor_copy(words[:], x_w[:].bitcast(U32).indirect(offset_columns(first, count)))
+            for done in range(0, count, CHUNK):
+                window = x_w[:].bitcast(U32).indirect(offset_columns(first + done, CHUNK))
+                nc.vector.tensor_copy(words[:, done : done + CHUNK], window)
             return [words[:, j : j + TILE] for j in range(0, count, TILE)]
 
         def permute_words(engine, words, raw):
@@ -163,13 +165,13 @@ def tile_moe_cas_glu_silu_kernel(
             )
             return words
 
-        def second_layer(n, half, words, bank):
-            cols = slice(half * HALF, (half + 1) * HALF)
+        def second_layer(n, half, words, bank, first=0, count=HALF):
+            cols = slice(half * HALF + first, half * HALF + first + count)
             nc.tensor.matmul_mx(
-                out=banks[bank][:],
+                out=banks[bank][:, 0:count],
                 lhsT=w2_w[:, n * P : (n + 1) * P].bitcast(FP8X4),
                 lhsT_scale=ws[:, N + n * P : N + (n + 1) * P],
-                rhs=words[:].bitcast(FP8X4),
+                rhs=words[:, first : first + count].bitcast(FP8X4),
                 rhs_scale=h_s[:, cols],
                 start=True,
                 stop=True,
@@ -197,27 +199,25 @@ def tile_moe_cas_glu_silu_kernel(
             nc.scalar.copy(*light_layer(0, piece * CHUNK, CHUNK, piece))
         nc.scalar.copy(*light_layer(0, 2 * BANK, BANK, 4))
         nc.scalar.copy(*light_layer(0, 3 * BANK, BANK, 5))
-        nc.scalar.copy(*light_layer(1, 0, BANK, 6))
-        silu(0, gate_sums(0, 7))
-        silu(1, gate_sums(1, 0))
-        product(0, value(0, 1))
-        product(1, value(1, 2))
-        silu(2, gate_sums(2, 3))
-        silu(3, gate_sums(3, 4))
-        product(2, value(2, 5))
+        silu(0, gate_sums(0, 6))
+        silu(1, gate_sums(1, 7))
+        product(0, value(0, 0))
+        product(1, value(1, 1))
+        silu(2, gate_sums(2, 2))
+        silu(3, gate_sums(3, 3))
+        product(2, value(2, 4))
         silu(4, gate_sums(4, 6))
-        product(3, value(3, 7))
-        silu(5, gate_sums(5, 0))
-        b4 = value(4, 1)
-        nc.scalar.copy(*light_layer(1, BANK, BANK, 3))
-        product(4, b4)
+        product(3, value(3, 5))
+        nc.scalar.copy(*light_layer(1, 0, BANK, 0))
+        silu(5, gate_sums(5, 7))
+        product(4, value(4, 1))
         first_half = quantise(0, "h_first")
-        silu(6, gate_sums(6, 4))
-        b5 = value(5, 2)
-        silu(7, gate_sums(7, 6))
+        silu(6, gate_sums(6, 2))
+        b5 = value(5, 4)
+        silu(7, gate_sums(7, 3))
         product(5, b5)
         product(6, value(6, 5))
-        product(7, value(7, 7))
+        product(7, value(7, 6))
         low = second_layer(0, 0, first_half, 0)
         z_a = keep.tile([P, CHUNK], F32, name="z_a", align_bytes=64)
         nc.scalar.copy(z_a[:], low[:, 0:CHUNK])
@@ -226,22 +226,24 @@ def tile_moe_cas_glu_silu_kernel(
         z_b = keep.tile([P, CHUNK], F32, name="gate7", align_bytes=64)
         nc.scalar.copy(z_b[:], low[:, CHUNK:HALF])
         scatter_on_vector(CHUNK, CHUNK, z_b[:])
-        nc.scalar.copy(*light_layer(1, 2 * BANK, BANK, 3))
-        high = second_layer(1, 0, first_half, 4)
+        nc.scalar.copy(*light_layer(1, BANK, BANK, 7))
+        nc.scalar.copy(*light_layer(1, 2 * BANK, BANK, 2))
+        high = second_layer(1, 0, first_half, 1)
         nc.scalar.copy(z_high[:, 0:CHUNK], high[:, 0:CHUNK])
-        nc.scalar.copy(*light_layer(1, 3 * BANK, BANK, 6))
+        nc.scalar.copy(*light_layer(1, 3 * BANK, BANK, 3))
         nc.scalar.copy(z_high[:, CHUNK:HALF], high[:, CHUNK:HALF])
         scatter_on_scalar(0, CHUNK)
-        low = second_layer(0, 1, second_half, 1)
-        high = second_layer(1, 1, second_half, 2)
+        low = second_layer(0, 1, second_half, 4, 0, CHUNK)
+        high = second_layer(1, 1, second_half, 6)
+        last = second_layer(0, 1, second_half, 5, CHUNK, CHUNK)
         z_c = keep.tile([P, HALF], F32, name="z_c", align_bytes=64)
-        nc.vector.tensor_copy(z_c[:, 0:CHUNK], low[:, 0:CHUNK])
-        nc.vector.tensor_copy(z_c[:, CHUNK:HALF], low[:, CHUNK:HALF])
+        nc.scalar.copy(z_c[:, 0:CHUNK], low[:, 0:CHUNK])
+        nc.vector.tensor_copy(z_c[:, CHUNK:HALF], last[:, 0:CHUNK])
+        nc.scalar.copy(z_high[:, HALF : HALF + CHUNK], high[:, 0:CHUNK])
+        nc.scalar.copy(z_high[:, HALF + CHUNK : S], high[:, CHUNK:HALF])
         scatter_on_vector(HALF, CHUNK, z_c[:, 0:CHUNK])
         scatter_on_vector(HALF + CHUNK, CHUNK, z_c[:, CHUNK:HALF])
         nc.sync.dma_start(out=out[0:P, :], in_=result[0][:])
-        nc.scalar.copy(z_high[:, HALF : HALF + CHUNK], high[:, 0:CHUNK])
-        nc.scalar.copy(z_high[:, HALF + CHUNK : S], high[:, CHUNK:HALF])
         scatter_on_scalar(CHUNK, LONG)
         scatter_on_scalar(CHUNK + LONG, LONG)
         nc.sync.dma_start(out=out[P : 2 * P, 0 : T // 2], in_=result[1][:, 0 : T // 2])

@@ -82,10 +82,12 @@ def tile_moe_cas_glu_silu_kernel(
         load_scales(nc.sync, x_s, 0, x_scales)
         load_scales(nc.sync, ws, 0, w_scales, range(0, 1))
         nc.sync.dma_start(out=x_w[:, 0:XA], in_=x_dram[:, 0:XA])
-        load_scales(nc.sync, ws, 0, w_scales, range(1, 4))
+        load_scales(nc.gpsimd, ws, 0, w_scales, range(3, 4))
+        load_scales(nc.sync, ws, 0, w_scales, range(1, 3))
+        load_scales(nc.sync, ws, 2 * N, w1_scales, range(0, 1))
         nc.sync.dma_start(out=x_w[:, XA:T], in_=x_dram[:, XA:T])
         load_words(nc.sync, w1_raw[:], w1_words)
-        load_scales(nc.sync, ws, 2 * N, w1_scales, range(0, 3))
+        load_scales(nc.sync, ws, 2 * N, w1_scales, range(1, 3))
         load_scales(nc.gpsimd, ws, 2 * N, w1_scales, range(3, 4))
         load_words(nc.sync, w3_raw[:], w3_words)
         load_scales(nc.gpsimd, w3s_raw, 0, w3_scales, range(3, 4))
@@ -96,11 +98,11 @@ def tile_moe_cas_glu_silu_kernel(
         def offset_columns(first, count):
             return offsets[:, first // PER_COLUMN : (first + count) // PER_COLUMN]
 
-        def gather_words(name, first, count):
+        def gather_words(name, first, count, piece):
             words = keep.tile([P, count], U32, name=name, align_bytes=64)
-            for done in range(0, count, CHUNK):
-                window = x_w[:].bitcast(U32).indirect(offset_columns(first + done, CHUNK))
-                nc.vector.tensor_copy(words[:, done : done + CHUNK], window)
+            for done in range(0, count, piece):
+                window = x_w[:].bitcast(U32).indirect(offset_columns(first + done, piece))
+                nc.vector.tensor_copy(words[:, done : done + piece], window)
             return [words[:, j : j + TILE] for j in range(0, count, TILE)]
 
         def permute_words(engine, words, raw):
@@ -188,12 +190,12 @@ def tile_moe_cas_glu_silu_kernel(
 
         nc.vector.tensor_copy(g_s[:], x_s[:].indirect(offsets[:]))
         permute_words(nc.vector, w1_w, w1_raw[:])
-        g_first = gather_words("g_first", 0, CHUNK)
+        g_first = gather_words("g_first", 0, 3 * TILE, 3 * TILE)
         permute_scales(nc.vector, w1_s, ws[:, 2 * N : 2 * N + H])
-        g_last = gather_words("g_last", 3 * CHUNK, CHUNK)
+        g_last = gather_words("g_last", 7 * TILE, TILE, TILE)
         permute_words(nc.vector, w3_w, w3_raw[:])
         permute_scales(nc.vector, w3_s, w3s_raw[:])
-        g_w = g_first + gather_words("stage", CHUNK, HALF) + g_last
+        g_w = g_first + gather_words("stage", 3 * TILE, HALF, CHUNK) + g_last
 
         for piece in range(4):
             nc.scalar.copy(*light_layer(0, piece * CHUNK, CHUNK, piece))
@@ -201,9 +203,9 @@ def tile_moe_cas_glu_silu_kernel(
         nc.scalar.copy(*light_layer(0, 3 * BANK, BANK, 5))
         silu(0, gate_sums(0, 6))
         silu(1, gate_sums(1, 7))
+        silu(2, gate_sums(2, 2))
         product(0, value(0, 0))
         product(1, value(1, 1))
-        silu(2, gate_sums(2, 2))
         silu(3, gate_sums(3, 3))
         product(2, value(2, 4))
         silu(4, gate_sums(4, 6))

@@ -82,12 +82,10 @@ def tile_moe_cas_glu_silu_kernel(
         load_scales(nc.sync, x_s, 0, x_scales)
         load_scales(nc.sync, ws, 0, w_scales, range(0, 1))
         nc.sync.dma_start(out=x_w[:, 0:XA], in_=x_dram[:, 0:XA])
-        load_scales(nc.gpsimd, ws, 0, w_scales, range(3, 4))
-        load_scales(nc.sync, ws, 0, w_scales, range(1, 3))
-        load_scales(nc.sync, ws, 2 * N, w1_scales, range(0, 1))
+        load_scales(nc.sync, ws, 0, w_scales, range(1, 4))
         nc.sync.dma_start(out=x_w[:, XA:T], in_=x_dram[:, XA:T])
         load_words(nc.sync, w1_raw[:], w1_words)
-        load_scales(nc.sync, ws, 2 * N, w1_scales, range(1, 3))
+        load_scales(nc.sync, ws, 2 * N, w1_scales, range(0, 3))
         load_scales(nc.gpsimd, ws, 2 * N, w1_scales, range(3, 4))
         load_words(nc.sync, w3_raw[:], w3_words)
         load_scales(nc.gpsimd, w3s_raw, 0, w3_scales, range(3, 4))
@@ -210,17 +208,17 @@ def tile_moe_cas_glu_silu_kernel(
         product(2, value(2, 4))
         silu(4, gate_sums(4, 6))
         product(3, value(3, 5))
-        nc.scalar.copy(*light_layer(1, 0, BANK, 0))
         silu(5, gate_sums(5, 7))
         product(4, value(4, 1))
         first_half = quantise(0, "h_first")
+        u5 = keep.tile([P, BANK], F32, name="u5", align_bytes=64)
+        nc.scalar.copy(by_token(u5[:]), value(5, 4))
+        nc.gpsimd.tensor_tensor(h[:, 5 * BANK : 6 * BANK], u5[:], gates[5][:], MULT)
         silu(6, gate_sums(6, 2))
-        b5 = value(5, 4)
         silu(7, gate_sums(7, 3))
-        product(5, b5)
         product(6, value(6, 5))
         product(7, value(7, 6))
-        low = second_layer(0, 0, first_half, 0)
+        low = second_layer(0, 0, first_half, 7)
         z_a = keep.tile([P, CHUNK], F32, name="z_a", align_bytes=64)
         nc.scalar.copy(z_a[:], low[:, 0:CHUNK])
         scatter_on_vector(0, CHUNK, z_a[:])
@@ -228,25 +226,25 @@ def tile_moe_cas_glu_silu_kernel(
         z_b = keep.tile([P, CHUNK], F32, name="gate7", align_bytes=64)
         nc.scalar.copy(z_b[:], low[:, CHUNK:HALF])
         scatter_on_vector(CHUNK, CHUNK, z_b[:])
-        nc.scalar.copy(*light_layer(1, BANK, BANK, 7))
+        nc.scalar.copy(*light_layer(1, 0, BANK, 0))
+        nc.scalar.copy(*light_layer(1, BANK, BANK, 4))
         nc.scalar.copy(*light_layer(1, 2 * BANK, BANK, 2))
         high = second_layer(1, 0, first_half, 1)
-        nc.scalar.copy(z_high[:, 0:CHUNK], high[:, 0:CHUNK])
+        nc.scalar.copy(z_high[:, 0:LONG], high[:, 0:LONG])
         nc.scalar.copy(*light_layer(1, 3 * BANK, BANK, 3))
-        nc.scalar.copy(z_high[:, CHUNK:HALF], high[:, CHUNK:HALF])
-        scatter_on_scalar(0, CHUNK)
-        low = second_layer(0, 1, second_half, 4, 0, CHUNK)
-        high = second_layer(1, 1, second_half, 6)
-        last = second_layer(0, 1, second_half, 5, CHUNK, CHUNK)
+        nc.scalar.copy(z_high[:, LONG:HALF], high[:, LONG:HALF])
+        scatter_on_scalar(0, LONG)
+        low = second_layer(0, 1, second_half, 5)
+        high = second_layer(1, 1, second_half, 1)
         z_c = keep.tile([P, HALF], F32, name="z_c", align_bytes=64)
-        nc.scalar.copy(z_c[:, 0:CHUNK], low[:, 0:CHUNK])
-        nc.vector.tensor_copy(z_c[:, CHUNK:HALF], last[:, 0:CHUNK])
+        nc.vector.tensor_copy(z_c[:, 0:CHUNK], low[:, 0:CHUNK])
+        nc.vector.tensor_copy(z_c[:, CHUNK:HALF], low[:, CHUNK:HALF])
         nc.scalar.copy(z_high[:, HALF : HALF + CHUNK], high[:, 0:CHUNK])
         nc.scalar.copy(z_high[:, HALF + CHUNK : S], high[:, CHUNK:HALF])
         scatter_on_vector(HALF, CHUNK, z_c[:, 0:CHUNK])
         scatter_on_vector(HALF + CHUNK, CHUNK, z_c[:, CHUNK:HALF])
         nc.sync.dma_start(out=out[0:P, :], in_=result[0][:])
-        scatter_on_scalar(CHUNK, LONG)
-        scatter_on_scalar(CHUNK + LONG, LONG)
+        scatter_on_scalar(LONG, LONG)
+        scatter_on_scalar(2 * LONG, CHUNK)
         nc.sync.dma_start(out=out[P : 2 * P, 0 : T // 2], in_=result[1][:, 0 : T // 2])
         nc.scalar.dma_start(out=out[P : 2 * P, T // 2 : T], in_=result[1][:, T // 2 : T])

@@ -199,23 +199,24 @@ def tile_moe_cas_glu_silu_kernel(
             nc.scalar.copy(*light_layer(0, piece * CHUNK, CHUNK, piece))
         nc.scalar.copy(*light_layer(0, 2 * BANK, BANK, 4))
         nc.scalar.copy(*light_layer(0, 3 * BANK, BANK, 5))
-        silu(0, gate_sums(0, 6))
-        silu(1, gate_sums(1, 7))
-        silu(2, gate_sums(2, 2))
-        product(0, value(0, 0))
-        product(1, value(1, 1))
-        silu(3, gate_sums(3, 3))
-        product(2, value(2, 4))
+        nc.scalar.copy(*light_layer(1, 0, BANK, 6))
+        silu(0, gate_sums(0, 7))
+        silu(1, gate_sums(1, 0))
+        silu(2, gate_sums(2, 1))
+        product(0, value(0, 2))
+        product(1, value(1, 3))
+        silu(3, gate_sums(3, 4))
+        product(2, value(2, 5))
         silu(4, gate_sums(4, 6))
-        product(3, value(3, 5))
-        silu(5, gate_sums(5, 7))
+        product(3, value(3, 7))
+        silu(5, gate_sums(5, 0))
         product(4, value(4, 1))
         first_half = quantise(0, "h_first")
         u5 = keep.tile([P, BANK], F32, name="u5", align_bytes=64)
-        nc.scalar.copy(by_token(u5[:]), value(5, 4))
+        nc.scalar.copy(by_token(u5[:]), value(5, 2))
         nc.gpsimd.tensor_tensor(h[:, 5 * BANK : 6 * BANK], u5[:], gates[5][:], MULT)
-        silu(6, gate_sums(6, 2))
-        silu(7, gate_sums(7, 3))
+        silu(6, gate_sums(6, 3))
+        silu(7, gate_sums(7, 4))
         product(6, value(6, 5))
         product(7, value(7, 6))
         low = second_layer(0, 0, first_half, 7)
@@ -226,25 +227,25 @@ def tile_moe_cas_glu_silu_kernel(
         z_b = keep.tile([P, CHUNK], F32, name="gate7", align_bytes=64)
         nc.scalar.copy(z_b[:], low[:, CHUNK:HALF])
         scatter_on_vector(CHUNK, CHUNK, z_b[:])
-        nc.scalar.copy(*light_layer(1, 0, BANK, 0))
-        nc.scalar.copy(*light_layer(1, BANK, BANK, 4))
+        nc.scalar.copy(*light_layer(1, BANK, BANK, 0))
         nc.scalar.copy(*light_layer(1, 2 * BANK, BANK, 2))
         high = second_layer(1, 0, first_half, 1)
-        nc.scalar.copy(z_high[:, 0:LONG], high[:, 0:LONG])
+        nc.scalar.copy(z_high[:, 0:CHUNK], high[:, 0:CHUNK])
         nc.scalar.copy(*light_layer(1, 3 * BANK, BANK, 3))
-        nc.scalar.copy(z_high[:, LONG:HALF], high[:, LONG:HALF])
-        scatter_on_scalar(0, LONG)
-        low = second_layer(0, 1, second_half, 5)
-        high = second_layer(1, 1, second_half, 1)
+        nc.scalar.copy(z_high[:, CHUNK:HALF], high[:, CHUNK:HALF])
+        scatter_on_scalar(0, CHUNK)
+        low = second_layer(0, 1, second_half, 5, 0, CHUNK)
+        high = second_layer(1, 1, second_half, 6)
+        last = second_layer(0, 1, second_half, 4, CHUNK, CHUNK)
         z_c = keep.tile([P, HALF], F32, name="z_c", align_bytes=64)
-        nc.vector.tensor_copy(z_c[:, 0:CHUNK], low[:, 0:CHUNK])
-        nc.vector.tensor_copy(z_c[:, CHUNK:HALF], low[:, CHUNK:HALF])
+        nc.scalar.copy(z_c[:, 0:CHUNK], low[:, 0:CHUNK])
+        nc.vector.tensor_copy(z_c[:, CHUNK:HALF], last[:, 0:CHUNK])
         nc.scalar.copy(z_high[:, HALF : HALF + CHUNK], high[:, 0:CHUNK])
         nc.scalar.copy(z_high[:, HALF + CHUNK : S], high[:, CHUNK:HALF])
         scatter_on_vector(HALF, CHUNK, z_c[:, 0:CHUNK])
         scatter_on_vector(HALF + CHUNK, CHUNK, z_c[:, CHUNK:HALF])
         nc.sync.dma_start(out=out[0:P, :], in_=result[0][:])
-        scatter_on_scalar(LONG, LONG)
-        scatter_on_scalar(2 * LONG, CHUNK)
+        scatter_on_scalar(CHUNK, LONG)
+        scatter_on_scalar(CHUNK + LONG, LONG)
         nc.sync.dma_start(out=out[P : 2 * P, 0 : T // 2], in_=result[1][:, 0 : T // 2])
         nc.scalar.dma_start(out=out[P : 2 * P, T // 2 : T], in_=result[1][:, T // 2 : T])

@@ -24,7 +24,7 @@ CHUNK = 256
 HALF = 512
 LONG = 384
 PER_COLUMN = 16
-XA = 1408
+XA = 1280
 
 
 def load_words(queue, tile, words):
@@ -82,10 +82,12 @@ def tile_moe_cas_glu_silu_kernel(
         load_scales(nc.sync, x_s, 0, x_scales)
         load_scales(nc.sync, ws, 0, w_scales, range(0, 1))
         nc.sync.dma_start(out=x_w[:, 0:XA], in_=x_dram[:, 0:XA])
-        load_scales(nc.sync, ws, 0, w_scales, range(1, 4))
+        load_scales(nc.gpsimd, ws, 0, w_scales, range(3, 4))
+        load_scales(nc.sync, ws, 0, w_scales, range(1, 3))
         nc.sync.dma_start(out=x_w[:, XA:T], in_=x_dram[:, XA:T])
+        load_scales(nc.sync, ws, 2 * N, w1_scales, range(0, 1))
         load_words(nc.sync, w1_raw[:], w1_words)
-        load_scales(nc.sync, ws, 2 * N, w1_scales, range(0, 3))
+        load_scales(nc.sync, ws, 2 * N, w1_scales, range(1, 3))
         load_scales(nc.gpsimd, ws, 2 * N, w1_scales, range(3, 4))
         load_words(nc.sync, w3_raw[:], w3_words)
         load_scales(nc.gpsimd, w3s_raw, 0, w3_scales, range(3, 4))

@@ -24,7 +24,7 @@ CHUNK = 256
 HALF = 512
 LONG = 384
 PER_COLUMN = 16
-XA = 1280
+XA = 1152
 
 
 def load_words(queue, tile, words):

@@ -167,13 +167,13 @@ def tile_moe_cas_glu_silu_kernel(
             )
             return words
 
-        def second_layer(n, half, words, bank, first=0, count=HALF):
-            cols = slice(half * HALF + first, half * HALF + first + count)
+        def second_layer(n, half, words, bank):
+            cols = slice(half * HALF, (half + 1) * HALF)
             nc.tensor.matmul_mx(
-                out=banks[bank][:, 0:count],
+                out=banks[bank][:],
                 lhsT=w2_w[:, n * P : (n + 1) * P].bitcast(FP8X4),
                 lhsT_scale=ws[:, N + n * P : N + (n + 1) * P],
-                rhs=words[:, first : first + count].bitcast(FP8X4),
+                rhs=words[:].bitcast(FP8X4),
                 rhs_scale=h_s[:, cols],
                 start=True,
                 stop=True,
@@ -232,22 +232,21 @@ def tile_moe_cas_glu_silu_kernel(
         nc.scalar.copy(*light_layer(1, BANK, BANK, 0))
         nc.scalar.copy(*light_layer(1, 2 * BANK, BANK, 2))
         high = second_layer(1, 0, first_half, 1)
-        nc.scalar.copy(z_high[:, 0:CHUNK], high[:, 0:CHUNK])
+        nc.scalar.copy(z_high[:, 0:LONG], high[:, 0:LONG])
         nc.scalar.copy(*light_layer(1, 3 * BANK, BANK, 3))
-        nc.scalar.copy(z_high[:, CHUNK:HALF], high[:, CHUNK:HALF])
-        scatter_on_scalar(0, CHUNK)
-        low = second_layer(0, 1, second_half, 5, 0, CHUNK)
-        high = second_layer(1, 1, second_half, 6)
-        last = second_layer(0, 1, second_half, 4, CHUNK, CHUNK)
+        nc.scalar.copy(z_high[:, LONG:HALF], high[:, LONG:HALF])
+        scatter_on_scalar(0, LONG)
+        low = second_layer(0, 1, second_half, 5)
+        high = second_layer(1, 1, second_half, 1)
         z_c = keep.tile([P, HALF], F32, name="z_c", align_bytes=64)
-        nc.scalar.copy(z_c[:, 0:CHUNK], low[:, 0:CHUNK])
-        nc.vector.tensor_copy(z_c[:, CHUNK:HALF], last[:, 0:CHUNK])
+        nc.vector.tensor_copy(z_c[:, 0:CHUNK], low[:, 0:CHUNK])
+        nc.vector.tensor_copy(z_c[:, CHUNK:HALF], low[:, CHUNK:HALF])
         nc.scalar.copy(z_high[:, HALF : HALF + CHUNK], high[:, 0:CHUNK])
         nc.scalar.copy(z_high[:, HALF + CHUNK : S], high[:, CHUNK:HALF])
         scatter_on_vector(HALF, CHUNK, z_c[:, 0:CHUNK])
         scatter_on_vector(HALF + CHUNK, CHUNK, z_c[:, CHUNK:HALF])
         nc.sync.dma_start(out=out[0:P, :], in_=result[0][:])
-        scatter_on_scalar(CHUNK, LONG)
-        scatter_on_scalar(CHUNK + LONG, LONG)
+        scatter_on_scalar(LONG, LONG)
+        scatter_on_scalar(2 * LONG, CHUNK)
         nc.sync.dma_start(out=out[P : 2 * P, 0 : T // 2], in_=result[1][:, 0 : T // 2])
         nc.scalar.dma_start(out=out[P : 2 * P, T // 2 : T], in_=result[1][:, T // 2 : T])

from contextlib import ExitStack

import concourse.mybir as mybir

K, T, S, H, N = 512, 2048, 1024, 512, 256
FLOPS = 2 * K * N * T + 2 * 2 * K * H * S + 2 * H * N * S

F32 = mybir.dt.float32
BF16 = mybir.dt.bfloat16
I32 = mybir.dt.int32
U32 = mybir.dt.uint32
U16 = mybir.dt.uint16
U8 = mybir.dt.uint8
FP8X4 = mybir.dt.float8_e4m3fn_x4
SILU = mybir.ActivationFunctionType.Silu
COPY = mybir.ActivationFunctionType.Copy
MULT = mybir.AluOpType.mult

P = 128
PACK = 4
BANK = 512
TILE = 128
CHUNK = 256
HALF = 512
LONG = 384
PER_COLUMN = 16
XA = 1152


def load_words(queue, tile, words):
    queue.dma_start(out=tile, in_=words[0].rearrange("p n d -> p (n d)").bitcast(I32))


def load_scales(queue, tile, first_col, scales, quadrants=range(4)):
    width = scales.shape[2]
    for q in quadrants:
        queue.dma_start(
            out=tile[32 * q : 32 * q + 4, first_col : first_col + width].bitcast(I32),
            in_=scales[0, 4 * q : 4 * q + 4, :].bitcast(I32),
        )


def tile_moe_cas_glu_silu_kernel(
    tc, x_words, x_scales, w_words, w_scales, w1_words, w1_scales, w3_words, w3_scales, w2_words, w2_scales, offs, out
):
    nc = tc.nc
    with ExitStack() as ctx:
        keep = ctx.enter_context(tc.tile_pool(name="keep", bufs=1))
        psum = ctx.enter_context(tc.psum_pool(name="psum", bufs=1))

        offsets = keep.tile([P, S // PER_COLUMN], U16, name="offsets")
        x_w = keep.tile([P, T], I32, name="x_w", align_bytes=64)
        x_s = keep.tile([P, T], U8, name="x_s", align_bytes=64)
        w_w = keep.tile([P, N], I32, name="w_w", align_bytes=64)
        w2_w = keep.tile([P, N], I32, name="w2_w", align_bytes=64)
        w1_raw = keep.tile([P, H], I32, name="w1_raw", align_bytes=64)
        w3_raw = keep.tile([P, H], I32, name="w3_raw", align_bytes=64)
        w1_w = keep.tile([P, H], I32, name="w1_w", align_bytes=64)
        w3_w = keep.tile([P, H], I32, name="w3_w", align_bytes=64)
        ws = keep.tile([P, 2 * N + H], U8, name="ws", align_bytes=64)
        w3s_raw = keep.tile([P, H], U8, name="stage", align_bytes=64)
        w1_s = keep.tile([P, H], U8, name="w1_s", align_bytes=64)
        w3_s = keep.tile([P, H], U8, name="w3_s", align_bytes=64)
        g_s = keep.tile([P, S], U8, name="g_s", align_bytes=64)
        h_s = keep.tile([P, S], U8, name="h_s", align_bytes=64)
        h = keep.tile([P, S * PACK], BF16, name="h", align_bytes=64)
        gates = [keep.tile([P, BANK], F32, name="gate%d" % j, align_bytes=64) for j in range(S // TILE)]
        banks = [psum.tile([P, BANK], F32, name="bank%d" % b) for b in range(8)]
        result = [keep.tile([P, T], F32, name="result%d" % n) for n in range(N // P)]
        z_high = keep.tile([P, S], F32, name="z_high", align_bytes=64)

        nc.vector.memset(x_s[:].bitcast(I32), 0)
        nc.vector.memset(ws[:].bitcast(I32), 0)
        nc.vector.memset(w3s_raw[:].bitcast(I32), 0)
        warm = keep.tile([P, 2], F32, name="warm")
        nc.vector.memset(warm[:, 0:1], 0.0)

        x_dram = x_words[0].rearrange("p n d -> p (n d)").bitcast(I32)
        nc.scalar.activation(warm[:, 1:2], warm[:, 0:1], SILU)
        nc.sync.dma_start(offsets[:], offs)
        load_words(nc.sync, w_w[:], w_words)
        load_scales(nc.sync, x_s, 0, x_scales)
        load_scales(nc.sync, ws, 0, w_scales, range(0, 1))
        nc.sync.dma_start(out=x_w[:, 0:XA], in_=x_dram[:, 0:XA])
        load_scales(nc.gpsimd, ws, 0, w_scales, range(3, 4))
        load_scales(nc.sync, ws, 0, w_scales, range(1, 3))
        nc.sync.dma_start(out=x_w[:, XA:T], in_=x_dram[:, XA:T])
        load_scales(nc.sync, ws, 2 * N, w1_scales, range(0, 1))
        load_words(nc.sync, w1_raw[:], w1_words)
        load_scales(nc.sync, ws, 2 * N, w1_scales, range(1, 3))
        load_scales(nc.gpsimd, ws, 2 * N, w1_scales, range(3, 4))
        load_words(nc.sync, w3_raw[:], w3_words)
        load_scales(nc.gpsimd, w3s_raw, 0, w3_scales, range(3, 4))
        load_scales(nc.sync, w3s_raw, 0, w3_scales, range(0, 3))
        load_scales(nc.sync, ws, N, w2_scales)
        load_words(nc.sync, w2_w[:], w2_words)

        def offset_columns(first, count):
            return offsets[:, first // PER_COLUMN : (first + count) // PER_COLUMN]

        def gather_words(name, first, count, piece):
            words = keep.tile([P, count], U32, name=name, align_bytes=64)
            for done in range(0, count, piece):
                window = x_w[:].bitcast(U32).indirect(offset_columns(first + done, piece))
                nc.vector.tensor_copy(words[:, done : done + piece], window)
            return [words[:, j : j + TILE] for j in range(0, count, TILE)]

        def permute_words(engine, words, raw):
            engine.tensor_copy(
                words[:].rearrange("p (t c i) -> p c t i", t=PACK, i=PACK),
                raw.rearrange("p (c i t) -> p c t i", t=PACK, i=PACK),
            )

        def permute_scales(engine, plane, raw):
            engine.tensor_copy(
                plane[:].rearrange("p (t m) -> p t m", t=PACK), raw.rearrange("p (m t) -> p t m", t=PACK)
            )

        def light_layer(n, first, count, bank):
            cols = slice(first, first + count)
            y = banks[bank][:, 0:count]
            nc.tensor.matmul_mx(
                out=y,
                lhsT=w_w[:, n * P : (n + 1) * P].bitcast(FP8X4),
                lhsT_scale=ws[:, n * P : (n + 1) * P],
                rhs=x_w[:, cols].bitcast(FP8X4),
                rhs_scale=x_s[:, cols],
                start=True,
                stop=True,
            )
            return result[n][:, cols], y

        def first_layer_sums(bank, words, plane, tile):
            sums = banks[bank][:].rearrange("p (t j) -> p t j", t=PACK)
            for t in range(PACK):
                nc.tensor.matmul_mx(
                    out=sums[:, t, :],
                    lhsT=words[:, t * P : (t + 1) * P].bitcast(FP8X4),
                    lhsT_scale=plane[:, t * P : (t + 1) * P],
                    rhs=g_w[tile].bitcast(FP8X4),
                    rhs_scale=g_s[:, tile * TILE : (tile + 1) * TILE],
                    start=True,
                    stop=True,
                )
            return sums.rearrange("p t j -> p j t")

        def by_token(columns):
            return columns.rearrange("p (j t) -> p j t", t=PACK)

        def gate_sums(tile, bank):
            return first_layer_sums(bank, w1_w, w1_s, tile)

        def silu(tile, a):
            nc.scalar.activation(by_token(gates[tile][:]), a, SILU)

        def value(tile, bank):
            return first_layer_sums(bank, w3_w, w3_s, tile)

        def product(tile, b):
            nc.vector.tensor_tensor(by_token(h[:, tile * BANK : (tile + 1) * BANK]), b, by_token(gates[tile][:]), MULT)

        def quantise(half, name):
            cols = slice(half * HALF, (half + 1) * HALF)
            words = keep.tile([P, HALF], U32, name=name, align_bytes=64)
            nc.vector.quantize_mx(
                out=words[:].bitcast(FP8X4), scales=h_s[:, cols], in_=h[:, half * HALF * PACK : (half + 1) * HALF * PACK]
            )
            return words

        def second_layer(n, half, words, bank):
            cols = slice(half * HALF, (half + 1) * HALF)
            nc.tensor.matmul_mx(
                out=banks[bank][:],
                lhsT=w2_w[:, n * P : (n + 1) * P].bitcast(FP8X4),
                lhsT_scale=ws[:, N + n * P : N + (n + 1) * P],
                rhs=words[:].bitcast(FP8X4),
                rhs_scale=h_s[:, cols],
                start=True,
                stop=True,
            )
            return banks[bank]

        def scatter_on_vector(first, count, z):
            nc.vector.tensor_copy(result[0][:].indirect(offset_columns(first, count)), z)

        def scatter_on_scalar(first, count):
            nc.scalar.activation(
                result[1][:].indirect(offset_columns(first, count)), z_high[:, first : first + count], COPY
            )

        nc.vector.tensor_copy(g_s[:], x_s[:].indirect(offsets[:]))
        permute_words(nc.vector, w1_w, w1_raw[:])
        g_first = gather_words("g_first", 0, 3 * TILE, 3 * TILE)
        permute_scales(nc.vector, w1_s, ws[:, 2 * N : 2 * N + H])
        g_last = gather_words("g_last", 7 * TILE, TILE, TILE)
        permute_words(nc.vector, w3_w, w3_raw[:])
        permute_scales(nc.vector, w3_s, w3s_raw[:])
        g_w = g_first + gather_words("stage", 3 * TILE, HALF, CHUNK) + g_last

        for piece in range(4):
            nc.scalar.copy(*light_layer(0, piece * CHUNK, CHUNK, piece))
        nc.scalar.copy(*light_layer(0, 2 * BANK, BANK, 4))
        nc.scalar.copy(*light_layer(0, 3 * BANK, BANK, 5))
        nc.scalar.copy(*light_layer(1, 0, BANK, 6))
        silu(0, gate_sums(0, 7))
        silu(1, gate_sums(1, 0))
        silu(2, gate_sums(2, 1))
        product(0, value(0, 2))
        product(1, value(1, 3))
        silu(3, gate_sums(3, 4))
        product(2, value(2, 5))
        silu(4, gate_sums(4, 6))
        product(3, value(3, 7))
        silu(5, gate_sums(5, 0))
        product(4, value(4, 1))
        first_half = quantise(0, "h_first")
        u5 = keep.tile([P, BANK], F32, name="u5", align_bytes=64)
        nc.scalar.copy(by_token(u5[:]), value(5, 2))
        nc.gpsimd.tensor_tensor(h[:, 5 * BANK : 6 * BANK], u5[:], gates[5][:], MULT)
        silu(6, gate_sums(6, 3))
        silu(7, gate_sums(7, 4))
        product(6, value(6, 5))
        product(7, value(7, 6))
        low = second_layer(0, 0, first_half, 7)
        z_a = keep.tile([P, CHUNK], F32, name="z_a", align_bytes=64)
        nc.scalar.copy(z_a[:], low[:, 0:CHUNK])
        scatter_on_vector(0, CHUNK, z_a[:])
        second_half = quantise(1, "h_second")
        z_b = keep.tile([P, CHUNK], F32, name="gate7", align_bytes=64)
        nc.scalar.copy(z_b[:], low[:, CHUNK:HALF])
        scatter_on_vector(CHUNK, CHUNK, z_b[:])
        nc.scalar.copy(*light_layer(1, BANK, BANK, 0))
        nc.scalar.copy(*light_layer(1, 2 * BANK, BANK, 2))
        high = second_layer(1, 0, first_half, 1)
        nc.scalar.copy(z_high[:, 0:LONG], high[:, 0:LONG])
        nc.scalar.copy(*light_layer(1, 3 * BANK, BANK, 3))
        nc.scalar.copy(z_high[:, LONG:HALF], high[:, LONG:HALF])
        scatter_on_scalar(0, LONG)
        low = second_layer(0, 1, second_half, 5)
        high = second_layer(1, 1, second_half, 1)
        z_c = keep.tile([P, HALF], F32, name="z_c", align_bytes=64)
        nc.vector.tensor_copy(z_c[:, 0:CHUNK], low[:, 0:CHUNK])
        nc.vector.tensor_copy(z_c[:, CHUNK:HALF], low[:, CHUNK:HALF])
        nc.scalar.copy(z_high[:, HALF : HALF + CHUNK], high[:, 0:CHUNK])
        nc.scalar.copy(z_high[:, HALF + CHUNK : S], high[:, CHUNK:HALF])
        scatter_on_vector(HALF, CHUNK, z_c[:, 0:CHUNK])
        scatter_on_vector(HALF + CHUNK, CHUNK, z_c[:, CHUNK:HALF])
        nc.sync.dma_start(out=out[0:P, :], in_=result[0][:])
        scatter_on_scalar(LONG, LONG)
        scatter_on_scalar(2 * LONG, CHUNK)
        nc.sync.dma_start(out=out[P : 2 * P, 0 : T // 2], in_=result[1][:, 0 : T // 2])
        nc.scalar.dma_start(out=out[P : 2 * P, T // 2 : T], in_=result[1][:, T // 2 : T])
